import numpy as np, ml_dtypes
CORES = [5,29,101,125,133,157,229,253]
N = 8
import mx_ref
BF = ml_dtypes.bfloat16
def pick(q, e):
    c = np.concatenate([q[0].reshape(128, -1, 4), np.zeros((128, 1, 4), np.uint8)], axis=1); s = np.concatenate([q[1], np.ones((16, 1), np.uint8)], axis=1)
    return (np.ascontiguousarray(c[:, e].reshape(128, -1)), np.ascontiguousarray(s[:, e]))
def join(*qs):
    return (np.concatenate([q[0] for q in qs], axis=1), np.concatenate([q[1] for q in qs], axis=1))
def put(q, e, v):
    c, s = q[0].reshape(128, -1, 4).copy(), q[1].copy(); c[:, e] = v[0].reshape(128, -1, 4); s[:, e] = v[1]
    return (c.reshape(128, -1), s)
def pk(c, s):
    return (np.ascontiguousarray(c), mx_ref.live(s))
def emit(q):
    return q[0], q[1]
def tile(rs):
    return np.stack(rs, axis=2).reshape(128, -1).astype(BF)
def cut(t, i, w=512):
    return t[:, w * i:w * i + w]
def f(rng, *shape):
    return mx_ref.flush((rng.standard_normal(shape, dtype=np.float32) * np.exp2(rng.integers(-2, 3, shape[:-1] + (1,)))).astype(BF))
def wide(rng, *shape, cols=0):
    v = rng.standard_normal(shape, dtype=np.float32) * np.exp2(rng.integers(-12, 13, shape)).astype(np.float32)
    if cols: v *= np.repeat(np.exp2(rng.integers(-cols, cols + 1, shape[:-2] + (1, shape[-1] // 4))) * (rng.random(shape[:-2] + (1, shape[-1] // 4)) > 0.0625), 4, axis=-1).astype(np.float32)
    return mx_ref.flush(v.astype(BF))
P, CAPP, L, CB = 128, 64, 3, 64
def big(v, k):
    v = v.astype(np.float32) * np.float32(k)
    v[np.abs(v) < np.float32(2.0 ** -10)] = 0
    return v.astype(BF)
def number(z):
    n = np.zeros(z.shape[1], np.int64)
    for b in range(L): n += (z[b] < 0) * (1 << b)
    return n
def buckets(x, pl):
    X = [mx_ref.quantize(np.ascontiguousarray(x[s])) for s in range(N)]
    return X, np.stack([number(mx_ref.matmul(mx_ref.quantize(np.ascontiguousarray(pl[s])), X[s])) for s in range(N)])
def taken(bk):
    at = np.full((N, N, CAPP), -1)
    for d in range(N):
        for s in range(N):
            e = np.flatnonzero(bk[s] == d)[:CAPP]
            at[d, s, :e.size] = e
    return at
def attend(c, wv, e):
    e = np.concatenate([e, np.setdiff1d(np.arange(512), e)[:max(4 - len(e), len(e) % 2)]])
    m = pick(c, e)
    ct = [pick(c, np.arange(t, 512, 4)) for t in range(4)]
    A = tile([np.float32(0.0625) * np.maximum(mx_ref.matmul(k, m) + np.float32(0), np.float32(0)) for k in ct])
    qw = mx_ref.quantize(np.ascontiguousarray(wv))
    V = tile([mx_ref.matmul(k, qw) for k in ct])
    qa = mx_ref.quantize(A)
    O = [mx_ref.matmul(mx_ref.quantize(np.ascontiguousarray(cut(V, i))), qa) for i in range(4)]
    h = np.zeros((128, 512, 4), BF)
    h[:, e] = tile([np.float32(0.0625) * o for o in O]).reshape(128, -1, 4)
    return A, V, h.reshape(128, 2048)
def planes(rng):
    p = np.array(f(rng, 128, 512))
    p[:, 4 * L:] = 0
    return np.stack([p] * N)
def plain(rng):
    return {"x": big(f(rng, N, 128, 4 * P), 0.25), "pl": planes(rng), "p2": planes(rng), "wv": big(f(rng, N, 128, 2048), 0.25), "w": f(rng, N, 128, 512)}
def aimed(rng, d, want, gone=0, then=None, two=None):
    x, p = d["x"].astype(np.float32).reshape(N, 128, P, 4), np.zeros((128, 128, 4), np.float32)
    gone = np.zeros((N, P), np.int64) + gone
    at = rng.permutation(128)[:16 * L + 16].reshape(L + 1, 16)
    side = np.zeros((N, 128, 4), np.float32)
    for b in range(L):
        v = (1 + rng.random((16, 4))) * rng.choice([-1.0, 1.0], (16, 4))
        p[at[b], b] = v
        turn = (1 - 2 * (want >> b & 1)) * (1 - (gone >> b & 1))
        x[:, at[b]] = np.abs(x[:, at[b]]) * (np.sign(v)[None, :, None, :] * turn[:, None, :, None]) * (0.0625 if then is None else 1.0)
        side[:, at[b]] = np.sign(v)[None] * (1 - 2 * (np.arange(N) >> b & 1))[:, None, None]
    parted = np.zeros((128, 4), np.float32)
    if two is not None:
        k = two[2][:, None, :, None]
        u = rng.choice([-1.0, 1.0], (16, 4))
        parted[at[L]] = u
        x = np.where(k != 0, np.float32(0.125) * x, x)
        x[:, at[L]] = np.where(k != 0, 0.5 * (1 + rng.random((N, 16, P, 4))) * u[None, :, None, :] * k, x[:, at[L]])
    x = x * (gone != N - 1)[:, None, :, None]
    d = {**d, "x": big(x.reshape(N, 128, 4 * P), 1), "pl": np.stack([p.reshape(128, 512).astype(BF)] * N)}
    if then is None: return d
    p2, wv = np.zeros((128, 128, 4), np.float32), d["wv"].astype(np.float32).reshape(N, 128, 4, 128, 4)
    on = rng.permutation(128)[:16 * L].reshape(L, 16)
    for b in range(L):
        p2[on[b], b] = 1 + rng.random((16, 4))
        for q in range(N):
            sign = parted if two is not None and q == two[0] and b == two[1] else side[q]
            wv[q][:, :, on[b]] = np.abs(wv[q][:, :, on[b]]) * sign[:, None, None, :] * (1 - 2 * (int(then[q]) >> b & 1))
    return {**d, "wv": big(wv.reshape(N, 128, 2048), 1), "p2": np.stack([p2.reshape(128, 512).astype(BF)] * N)}
def setup_inputs(rng):
    return plain(rng)
def setup_inputs_crowd(rng):
    h, g = (int(v) for v in rng.permutation(N)[:2])
    c, then = rng.permutation(N), np.zeros(N, np.int64)
    then[c] = np.roll(c, 1)
    bit = int(rng.choice([b for b in range(L) if int(then[h]) ^ (1 << b) != h]))
    one = int(rng.choice([q for q in range(N) if q not in (h, g) and int(then[q]) != int(then[h]) ^ (1 << bit)]))
    others = np.delete(np.arange(N), [h, g, one])
    o, n = rng.permutation(N), np.full(N, CAPP)
    n[o[N // 2:]] += rng.integers(1, P - CAPP + 1, N - N // 2)
    n[o[-1]] = P
    r, more = int(o[N // 2]), P // (CAPP + 1) - 1
    if more: n[r] = rng.integers(CAPP + 1, P - more * (CAPP + 1) + 1)
    want = rng.choice(others, (N, P))
    for s in range(N): want[s, rng.permutation(P)[:n[s]]] = h
    e = rng.permutation(np.flatnonzero((want != h) & (np.arange(N) != r)[:, None]))
    want.flat[e[:CB]] = g
    want.flat[e[CB]] = one
    if more:
        e = rng.permutation(np.flatnonzero(want[r] != h))
        want[r, e[:more * (CAPP + 1)]] = np.repeat(rng.choice(others, more, replace=False), CAPP + 1)
    kind = np.zeros((N, P), np.int64)
    for s in range(N):
        e = np.flatnonzero(want[s] == h)
        kind[s, e] = 1 - 2 * ((np.arange(e.size) + int(rng.integers(0, 2))) % 2)
    return aimed(rng, plain(rng), want, then=then, two=(h, bit, kind))
def setup_inputs_few(rng):
    o = rng.permutation(N)
    want = rng.choice(o[2:], (N, P))
    want[int(rng.integers(0, N)), int(rng.integers(0, P))] = o[0]
    return aimed(rng, plain(rng), want)
def setup_inputs_neg(rng):
    d, g = plain(rng), rng.permutation(16)
    want = np.stack([rng.permutation(P) % N for s in range(N)])
    part = 8 * g[:, None] + np.arange(8)
    rows = (4 * part[L:].reshape(-1)[:, None] + np.arange(4)).reshape(-1)
    x, p = np.zeros((N, P, 512)), np.zeros((128, 128, 4))
    for b in range(L):
        v = rng.choice([-1.0, 1.0], (8, 4))
        p[part[b], b] = v * (1 + rng.random((8, 4)))
        e = (4 * part[b][:, None] + np.arange(4)).reshape(-1)
        x[:, :, e] = 2.0 ** -8 * v.reshape(-1) * (1 - 2 * (want >> b & 1))[:, :, None]
    for q in range(N):
        s, i = np.nonzero(want == q)
        v = np.full((P, P), -2.0 ** -7)
        v[np.arange(P), np.arange(P)] = P * 2.0 ** -7
        x[s[:, None], i[:, None], rng.permutation(rows)[:P][None, :]] = v * rng.choice([-1.0, 1.0], P)
    x *= np.exp2(rng.integers(-1, 2, (N, P, 1)))
    x = np.ascontiguousarray(x.reshape(N, P, 128, 4).transpose(0, 2, 1, 3)).reshape(N, 128, 4 * P)
    return {**d, "x": x.astype(np.float32).astype(BF), "pl": np.stack([p.reshape(128, 512).astype(np.float32).astype(BF)] * N)}
def setup_inputs_zero(rng):
    gone = np.zeros((N, P), np.int64)
    for s in range(N):
        e = rng.permutation(P)
        gone[s, e[:P // 4]] = N - 1
        gone[s, e[P // 4:P // 2]] = 1 << rng.integers(0, L, P // 2 - P // 4)
    d = aimed(rng, plain(rng), rng.integers(0, N, (N, P)), gone)
    b, q, on = int(rng.integers(0, L)), int(rng.integers(0, N)), rng.permutation(128)[:16]
    p2, wv = np.array(d["p2"]).reshape(N, 128, 128, 4), np.array(d["wv"]).reshape(N, 128, 4, 128, 4)
    p2[:, np.setdiff1d(np.arange(128), on), b] = 0
    wv[q][:, :, on] = 0
    return {**d, "p2": p2.reshape(N, 128, 512), "wv": wv.reshape(N, 128, 2048)}
def setup_inputs_spread(rng):
    return {**plain(rng), "x": big(wide(rng, N, 128, 4 * P, cols=2), 2.0 ** -10)}
def check_inputs(d):
    b = []
    for k in ("x", "pl", "p2", "wv", "w"):
        v = np.abs(d[k].astype(np.float32))
        if not (np.isfinite(v).all() and ((v == 0) | (v >= 2.0 ** -30) & (v <= 2.0 ** 30)).all()): b.append("a value of " + k)
    for k in ("pl", "p2"):
        p = d[k].astype(np.float32)
        if (p[:, :, 4 * L:] != 0).any(): b.append(k + " has numbers behind its first L columns")
        if (p != p[:1]).any(): b.append(k + " isn't the same on all ranks")
    return b
def reference(x, pl, p2, wv, w):
    X, bk = buckets(x, pl)
    at = taken(bk)
    H, num, to = [], [], []
    for d in range(N):
        c = join(*[pick(X[s], at[d, s]) for s in range(N)])
        A, V, h = attend(c, wv[d], np.flatnonzero(at[d].reshape(-1) >= 0))
        h = mx_ref.quantize(h)
        n = np.concatenate([np.where(at[d, s] >= 0, P * s + at[d, s], -1) for s in range(N)])
        H.append(h)
        num.append(n)
        to.append(np.where(n >= 0, number(mx_ref.matmul(mx_ref.quantize(np.ascontiguousarray(p2[d])), h)), -1))
    H = join(*H)
    num = np.concatenate(num + [np.full(1, -1)])
    oc, osc = np.zeros((N, 128, 4 * N * CB), np.uint8), np.zeros((N, 16, N * CB), np.uint8)
    nb, y = np.zeros((N, 1, N * CB), np.float32), np.zeros((N, 128, N * CB), np.float32)
    for e in range(N):
        k = np.full(N * CB, -1)
        for d in range(N):
            i = np.flatnonzero(to[d] == e)[:CB]
            k[d * CB + np.arange(i.size)] = 512 * d + i
        h = pick(H, k)
        oc[e], osc[e] = emit(h)
        nb[e, 0] = num[k]
        y[e] = mx_ref.matmul(mx_ref.quantize(np.ascontiguousarray(w[e])), h)
    return {"oc": oc, "osc": osc, "id": nb, "y": y}

@@ -1,0 +1,459 @@
+from concourse.bass import DstId, RemoteDMATransfer
+from concourse.mybir import dt, AluOpType as OP, AxisListType, ActivationFunctionType as AF
+
+F8, U8, BF, F32, U16, I32 = "float8_e4m3fn_x4", "uint8", "bfloat16", "float32", "uint16", "int32"
+SCRATCH = {"ps": ("psum", [128, 4096], F32)}
+for _n, _w in (("xq", 130), ("plq", 128), ("p2q", 128), ("wq", 128), ("wvq", 512), ("sl1r", 256), ("sl1d", 192), ("cl", 512),
+               ("cp", 512), ("vq", 512), ("aq", 512), ("hq", 640), ("sl2r", 256), ("sl2d", 192), ("hl", 512),
+               ("r1", 64), ("r2", 64)):
+    SCRATCH[_n + "c"] = ("sbuf", [128, _w], F8)
+    SCRATCH[_n + "s"] = ("sbuf", [128, _w], U8)
+for _t, _b in ((BF, "xt 520 plt 512 p2t 512 wt 512 wvt 2048 zt 512 vt 2048 at 2048 ht 2048 vals 256 bs1 128 tr1 128 e1 128 m1 128 "
+                    "s1 128 jS 2048 jV 2048 lst1 16 ll1 16 bs2 512 tr2 512 e32 512 e8 128 m2 512 s2 512 t2 512 rr 128 ra 64 rb 32 "
+                    "win 784 ta 512 tb 544 wm 34 r1l 2"),
+               (F32, "cf 4 wc 8 wcol 8 mE 8 i16 16 u16 8 thr 16 addc 8 kc1 128 l32x 8 i8 8 l4x 8 ic 32 p16 8 iv 256 idu 16 dump 16 "
+                     "idc 16 ny1 8 num1 8 x1 32 x1t 32 la 16 lb 16 lf 16 inv 16 idx 512 idrow 520 nx 16 ny 16 num2 16 rc 16 n64 16 "
+                     "ov 16 su 16 sv 16 sw 16 x2 32 y2 32 z2 32 idg 512 idt 512 idm 8 idl 8 ysb 512 r2l 1"),
+               (U16, "rep1 8 offdb 8 offc 32 offs1 32 sc 16 offs2 32"), (I32, "pI 2 ci 4")):
+    _b = _b.split()
+    for _i in range(0, len(_b), 2):
+        SCRATCH[_b[_i]] = ("sbuf", [128, int(_b[_i + 1])], _t)
+SEMAPHORES = ("pv psc pt pg ldx ldpl ldwv ldp2 ldw a1 l1 a2d a2r l2d l2r ls st sts rc1 rs1 rl1 rc2 rs2 rl2").split()
+
+
+def kmap(topo, cores, s):
+    far = [d for d in range(8) if d != s and not topo.may_write(cores[s], cores[d])]
+    for w in ((1, 2, 4), (1, 4, 2), (2, 1, 4), (2, 4, 1), (4, 1, 2), (4, 2, 1)):
+        for f in range(8):
+            k = [sum(w[b] * ((d >> b ^ f >> b) & 1) for b in range(3)) for d in range(8)]
+            if k[s] == 7 and all(k[d] < 4 for d in far):
+                return w, f, k, [k.index(i) for i in range(8)], far
+    raise ValueError("no order of the destinations")
+
+
+def relays(topo, cores, s):
+    far = kmap(topo, cores, s)[4]
+    return [c for c in topo.cores_of(cores[s]) if c != cores[s] and all(topo.may_write(c, cores[d]) for d in far)]
+
+
+def bits(es):
+    return sum(1 << e for e in es)
+
+
+def near_engines(topo, cores, s, d, scales=False):
+    es = topo.engines(cores[s], cores[d])
+    i = kmap(topo, cores, s)[2][d] - 4
+    return ((es[0:4], es[4:6], es[6:8]) if scales else (es[0:2], es[2:4], es[4:8]))[i]
+
+
+def relay_program(g, core, T, topo):
+    C = T.cores
+    for s in range(8):
+        if core not in topo.cores_of(C[s]):
+            continue
+        rl = relays(topo, C, s)
+        if core not in rl[:4]:
+            continue
+        d = kmap(topo, C, s)[3][rl.index(core)]
+        rid, pid = topo.addr(C[d], core)
+        es = topo.engines(core, C[d])
+
+        def go(sem, n, out, src, rsem):
+            g.wait_ge(T.sem[sem], n)
+            g.remote_dma(out, src, T.sem[rsem], T.sem.ls, pid, rid, bits(es))
+        a, b = 64 * s, 64 * s + 64
+        go("rc1", 4, T.clc[:, a:b].bitcast(dt.uint8), T.r1c[:, 0:64].bitcast(dt.uint8), "a1")
+        go("rs1", 4, T.cls[:, a:b], T.r1s[:, 0:64], "a1")
+        go("rl1", 2, T.ll1[:, 2 * s:2 * s + 2], T.r1l[:, 0:2], "l1")
+        go("rc2", 4, T.hlc[:, a:b].bitcast(dt.uint8), T.r2c[:, 0:64].bitcast(dt.uint8), "a2r")
+        go("rs2", 4, T.hls[:, a:b], T.r2s[:, 0:64], "a2r")
+        go("rl2", 2, T.idl[:, s:s + 1], T.r2l[:, 0:1], "l2r")
+        g.wait_ge(T.sem.ls, 6 * len(es))
+
+
+def rank_program(g, core, T, topo):
+    me = T.rank_of(core)
+    if me is None:
+        return relay_program(g, core, T, topo)
+    C = T.cores
+    w3, flip, kof, dof, far = kmap(topo, C, me)
+    near = [d for d in range(8) if d != me and d not in far]
+    K0 = sum(w3[b] for b in range(3) if flip >> b & 1)
+    rl = relays(topo, C, me)
+    Q = {"v": g.vector, "s": g.scalar, "t": g.tensor, "g": g, "y": g.sync}
+    SEM = {"v": "pv", "s": "psc", "t": "pt", "g": "pg"}
+    cnt, seen = {}, {q: {} for q in Q}
+
+    def W(q, *toks):
+        best = {}
+        for t in toks:
+            best[t[0]] = max(best.get(t[0], 0), t[1])
+        for sem in best:
+            if seen[q].get(sem, 0) < best[sem]:
+                Q[q].wait_ge(T.sem[sem], best[sem])
+                seen[q][sem] = best[sem]
+
+    def done(q, inst):
+        cnt[q] = cnt.get(q, 0) + 1
+        inst.then_inc(T.sem[SEM[q]], 1)
+        return (SEM[q], cnt[q])
+
+    def V(inst):
+        return done("v", inst)
+
+    def S(inst):
+        return done("s", inst)
+
+    def load(q, sem, out, in_):
+        cnt[sem] = cnt.get(sem, 0) + 16
+        Q[q].dma_start(out, in_).then_inc(T.sem[sem], 16)
+        return (sem, cnt[sem])
+    v, sc, te = g.vector, g.scalar, g.tensor
+
+    def C1(k, inst):
+        return V(inst)
+
+    ldx = load("y", "ldx", T.xt[:, 0:512], T.x[:])
+    ldpl = load("s", "ldpl", T.plt[:, 0:128], T.pl[:, 0:128])
+    W("y", ldx)
+    ldwv = load("y", "ldwv", T.wvt[:], T.wv[:])
+    ldp2 = load("y", "ldp2", T.p2t[:, 0:128], T.p2[:, 0:128])
+    ldw = load("y", "ldw", T.wt[:], T.w[:])
+
+    fl = {"allow_small_or_imprecise_dtypes": True}
+    gi = done("g", g.iota(T.pI[:, 0:1], [[0, 1]], 0, 1))
+    done("g", g.iota(T.kc1[:], [[0, 4], [1, 8], [0, 4]], -K0, 0, **fl))
+    gi2 = done("g", g.iota(T.i16[:], [[1, 16]], 0, 0, **fl))
+    done("g", g.iota(T.i8[:], [[1, 8]], 0, 0, **fl))
+    done("g", g.iota(T.ic[:], [[1, 4], [64, 8]], 0, 0, **fl))
+    done("g", g.iota(T.iv[:], [[32, 16], [1, 16]], -256, 0, **fl))
+    done("g", g.iota(T.idu[:], [[16, 16]], 512, 0, **fl))
+    gi3 = done("g", g.iota(T.idc[:], [[128, 8], [0, 2]], 0, 0, **fl))
+    zx = V(v.memset(T.xt[:, 512:520], 0.0))
+    for b in range(4):
+        rep1 = V(v.memset(T.rep1[:, 2 * b:2 * b + 2], b))
+    W("v", gi)
+    V(v.tensor_scalar(T.ci[:, 0:1], T.pI[:, 0:1], 31, None, OP.bitwise_and))
+    V(v.tensor_scalar(T.ci[:, 1:2], T.pI[:, 0:1], 15, None, OP.bitwise_and))
+    V(v.tensor_scalar(T.ci[:, 2:3], T.pI[:, 0:1], 4, 1, OP.arith_shift_right, OP.bitwise_and))
+    c0 = V(v.tensor_scalar(T.ci[:, 3:4], T.pI[:, 0:1], 3, None, OP.bitwise_and))
+    W("v", c0)
+    c0 = V(v.tensor_copy(T.cf[:], T.ci[:]))
+    W("v", c0)
+    lane, l16, mO, u4 = (T.cf[:, i:i + 1] for i in range(4))
+    for b in range(3):
+        c1 = V(v.tensor_scalar(T.wc[:, b:b + 1], lane, float(b), float(-w3[b] if flip >> b & 1 else w3[b]), OP.is_equal, OP.mult))
+    c2 = V(v.tensor_scalar(T.u16[:, 0:1], u4, 16.0, 0.5, OP.mult, OP.add))
+    nS = 9
+    c3 = V(v.tensor_scalar(T.addc[:, 0:1], l16, nS - 0.5, 64.0, OP.is_lt, OP.mult))
+    c4 = V(v.tensor_scalar(T.mE[:, 0:1], mO, -1.0, 1.0, OP.mult, OP.add))
+    W("v", c1)
+    c1 = V(v.tensor_tensor(T.wc[:, 3:4], T.wc[:, 0:1], T.wc[:, 1:2], OP.add))
+    W("v", c1)
+    wc = V(v.tensor_tensor(T.wcol[:, 0:1], T.wc[:, 3:4], T.wc[:, 2:3], OP.add))
+    W("v", c2, gi2)
+    thr = V(v.tensor_scalar(T.thr[:], T.i16[:], T.u16[:, 0:1], None, OP.add))
+    wcol, mE = T.wcol[:, 0:1], T.mE[:, 0:1]
+
+    W("v", ldpl)
+    for a in range(1, 4):
+        k = V(v.tensor_copy(T.plt[:, 128 * a:128 * a + 128], T.plt[:, 0:128]))
+    W("v", k)
+    qpl = V(v.quantize_mx(T.plqc[:, 0:128], T.plqs[:, 0:128], T.plt[:, 0:512]))
+    W("v", ldx, zx)
+    qx = V(v.quantize_mx(T.xqc[:, 0:130], T.xqs[:, 0:130], T.xt[:, 0:520]))
+
+    def mm(out, n, l, lo, r, ro):
+        return done("t", te.matmul_mx(T.ps[:, out:out + n], T[l + "c"][:, lo:lo + 128], T[l + "s"][:, lo:lo + 128],
+                                      T[r + "c"][:, ro:ro + n], T[r + "s"][:, ro:ro + n], True, True))
+    W("t", qpl, qx)
+    z = mm(0, 128, "plq", 0, "xq", 0)
+    W("v", z, wc)
+    z1 = V(v.tensor_scalar(T.bs1[:], T.ps[:, 0:128], 0.0, wcol, OP.is_lt, OP.mult))
+    W("v", z1)
+    k = V(v.transpose(T.tr1[:], T.bs1[:]))
+    W("v", k)
+    k = V(v.tensor_tensor(T.ny1[:, 0:4], T.tr1[:, 1:128:32], T.tr1[:, 2:128:32], OP.add))
+    W("v", k)
+    k = V(v.tensor_tensor(T.num1[:, 0:4], T.tr1[:, 0:128:32], T.ny1[:, 0:4], OP.add))
+    W("v", k, rep1, gi2)
+    k = V(v.tensor_tensor(T.e1[:], T.num1[:, 0:4].indirect(T.rep1[:, 0:8]), T.kc1[:], OP.is_equal))
+    W("v", k)
+    k = V(v.transpose(T.m1[:], T.e1[:]))
+    W("v", k)
+    k = V(v.tensor_tensor_scan(T.s1[:], T.m1[:], T.m1[:], 0.0, OP.add, OP.max))
+    W("s", k, thr)
+    W("v", k, thr)
+    for i in range(nS):
+        ks = S(sc.activation(T.jS[:, 128 * i:128 * i + 128], T.s1[:], AF.Sign, bias=T.thr[:, i:i + 1], scale=-1.0, accum_out=T.x1[:, i:i + 1]))
+    cs = [V(v.tensor_scalar(T.jV[:, 128 * i:128 * i + 128], T.s1[:], T.thr[:, i:i + 1], 2.0, OP.is_lt, OP.mult)) for i in range(nS, 16)]
+    for i in range(nS, 16):
+        W("v", cs[i - nS])
+        k = V(v.tensor_reduce(T.x1[:, i:i + 1], T.jV[:, 128 * i:128 * i + 128], AxisListType.X, OP.add))
+    W("v", k, ks)
+    k = V(v.tensor_copy(T.x1[:, 16:32], T.x1[:, 0:16]))
+    W("v", k)
+    k = V(v.transpose(T.x1t[:], T.x1[:]))
+    W("v", k, c3)
+    of1 = V(v.tensor_scalar(T.offs1[:], T.x1t[:], 0.5, T.addc[:, 0:1], OP.mult, OP.add))
+    W("v", of1)
+    W("s", of1)
+
+    def pickc(out, a, b, src, n, off, e, f):
+        return V(v.tensor_copy(T[out + "c"][:, a:b].bitcast(dt.uint32), T[src + "c"][:, 0:n].bitcast(dt.uint32).indirect(T[off][:, e:f])))
+
+    def picks(out, a, b, src, n, off, e, f):
+        return S(sc.activation(T[out + "s"][:, a:b], T[src + "s"][:, 0:n].indirect(T[off][:, e:f]), AF.Copy))
+    own = 64 * me
+    c1r = pickc("sl1r", 0, 256, "xq", 130, "offs1", 0, 16)
+    s1r = picks("sl1r", 0, 256, "xq", 130, "offs1", 0, 16)
+    c1d = pickc("sl1d", 0, 192, "xq", 130, "offs1", 16, 28)
+    s1d = picks("sl1d", 0, 192, "xq", 130, "offs1", 16, 28)
+    c1o = pickc("cl", own, own + 64, "xq", 130, "offs1", 28, 32)
+    s1o = picks("cl", own, own + 64, "xq", 130, "offs1", 28, 32)
+    W("v", c4)
+    V(v.tensor_scalar(T.la[:], T.offs1[:, 0:32:2], mE, None, OP.mult))
+    k = V(v.tensor_scalar(T.lb[:], T.offs1[:, 1:32:2], mO, None, OP.mult))
+    W("v", k)
+    l1 = V(v.tensor_tensor(T.lst1[:], T.la[:], T.lb[:], OP.add))
+
+    lsn = [0]
+
+    def fused(parts):
+        tr = []
+        for dst, es, s_, d_, sem in parts:
+            rid, pid = topo.addr(dst, core)
+            tr.append(RemoteDMATransfer(dst_ids=[DstId(rid=rid, pnc=pid)], dma_engine_mask=bits(es), remote_sem=T.sem[sem], srcs=[s_], dsts=[d_]))
+            lsn[0] += len(es)
+        g.remote_dma_fused(tr, local_sem=T.sem.ls)
+
+    def far_parts(src, dst, sem, lst=False):
+        es = [topo.engines(core, c) for c in rl[:4]]
+        return [(rl[i], es[i][8 + 2 * i:10 + 2 * i] if lst else es[i][4 * i:4 * i + 4], src(i), dst, sem) for i in range(4)]
+
+    def near_parts(src, dst, sem, scales=False):
+        return [(C[dof[4 + i]], near_engines(topo, C, me, dof[4 + i], scales), src(i), dst, sem) for i in range(3)]
+
+    def u8(t, a, b):
+        return T[t][:, a:b].bitcast(dt.uint8)
+    W("g", c1r)
+    fused(far_parts(lambda i: u8("sl1rc", 64 * i, 64 * i + 64), u8("r1c", 0, 64), "rc1"))
+    W("g", s1r)
+    fused(far_parts(lambda i: T.sl1rs[:, 64 * i:64 * i + 64], T.r1s[:, 0:64], "rs1"))
+    W("g", c1d)
+    fused(near_parts(lambda i: u8("sl1dc", 64 * i, 64 * i + 64), u8("clc", own, own + 64), "a1"))
+    W("g", s1d)
+    fused(near_parts(lambda i: T.sl1ds[:, 64 * i:64 * i + 64], T.cls[:, own:own + 64], "a1", True))
+    W("g", l1)
+    fused(far_parts(lambda i: T.lst1[:, 2 * i:2 * i + 2], T.r1l[:, 0:2], "rl1", True))
+    fused(near_parts(lambda i: T.lst1[:, 8 + 2 * i:10 + 2 * i], T.ll1[:, 2 * me:2 * me + 2], "l1"))
+
+    W("v", gi3, c0)
+    V(v.tensor_scalar(T.l32x[:, 0:1], l16, 32.0, None, OP.mult))
+    V(v.tensor_scalar(T.p16[:, 0:1], mO, 16.0, None, OP.mult))
+    k = V(v.tensor_scalar(T.l4x[:, 0:1], l16, 4.0, None, OP.mult))
+    W("v", k)
+    oc_ = V(v.tensor_scalar(T.offc[:], T.ic[:], T.l4x[:, 0:1], None, OP.add))
+    W("v", ldwv)
+    qwv = V(v.quantize_mx(T.wvqc[:, 0:512], T.wvqs[:, 0:512], T.wvt[:, 0:2048]))
+    V(v.tensor_scalar(T.offdb[:], T.i8[:], T.l32x[:, 0:1], None, OP.add))
+    V(v.tensor_scalar(T.vals[:], T.iv[:], T.p16[:, 0:1], None, OP.add))
+    V(v.tensor_scalar(T.dump[:], T.idu[:], l16, None, OP.add))
+    V(v.memset(T.win[:], 256.0))
+    V(v.memset(T.e32[:], 0.0))
+    V(v.memset(T.idx[:], 0.0))
+    V(v.memset(T.idrow[:, 512:520], -1.0))
+    V(v.memset(T.idm[:], 0.0))
+    W("v", ldp2)
+    for a in range(1, 4):
+        V(v.tensor_copy(T.p2t[:, 128 * a:128 * a + 128], T.p2t[:, 0:128]))
+    k = V(v.memset(T.zt[:], 0.0))
+    W("v", k, ldw)
+    V(v.quantize_mx(T.hqc[:, 512:640], T.hqs[:, 512:640], T.zt[:, 0:512]))
+    qp2 = V(v.quantize_mx(T.p2qc[:, 0:128], T.p2qs[:, 0:128], T.p2t[:, 0:512]))
+    qw = V(v.quantize_mx(T.wqc[:, 0:128], T.wqs[:, 0:128], T.wt[:, 0:512]))
+
+    nd, ndl, nf = 0, 0, 0
+    for s in range(8):
+        if s in far:
+            nf += len(topo.engines(relays(topo, C, s)[kmap(topo, C, s)[2][me]], core))
+        elif s != me:
+            ndl += len(near_engines(topo, C, s, me))
+            nd += len(near_engines(topo, C, s, me)) + len(near_engines(topo, C, s, me, True))
+    a1 = ("a1", nd + 2 * nf)
+    W("v", a1, c1o, s1o, oc_)
+    W("s", a1, c1o, s1o, oc_)
+    W("t", a1, c1o, s1o, qwv)
+    pc, pp = [], []
+    for t in range(4):
+        pc.append(pickc("cp", 128 * t, 128 * t + 128, "cl", 512, "offc", 8 * t, 8 * t + 8))
+        pp.append(picks("cp", 128 * t, 128 * t + 128, "cl", 512, "offc", 8 * t, 8 * t + 8))
+    vc, al, ar = [], [], []
+    for t in range(4):
+        W("t", pc[t], pp[t], z1)
+        m = mm(512 * t, 512, "cp", 128 * t, "wvq", 0)
+        W("v", m)
+        vc.append(V(v.tensor_copy(T.vt[:, t:2048:4], T.ps[:, 512 * t:512 * t + 512])))
+    for h, acc in ((0, al), (1, ar)):
+        for t in range(4):
+            if h:
+                W("t", al[t])
+            m = mm(2048 + 512 * t, 256, "cp", 128 * t, "cl", 256 * h)
+            W("s", m)
+            acc.append(S(sc.activation(T["at"][:, 1024 * h + t:1024 * h + 1024:4], T.ps[:, 2048 + 512 * t:2304 + 512 * t], AF.Relu, scale=0.0625)))
+    W("v", *vc)
+    qv = V(v.quantize_mx(T.vqc[:, 0:512], T.vqs[:, 0:512], T.vt[:, 0:2048]))
+    W("v", *al)
+    qa = [V(v.quantize_mx(T.aqc[:, 0:256], T.aqs[:, 0:256], T["at"][:, 0:1024]))]
+    W("v", ("l1", ndl + nf), l1)
+    if me > 0:
+        V(v.tensor_copy(T.lf[:, 0:2 * me], T.ll1[:, 0:2 * me]))
+    if me < 7:
+        V(v.tensor_copy(T.lf[:, 2 * me + 2:16], T.ll1[:, 2 * me + 2:16]))
+    k = V(v.tensor_copy(T.lf[:, 2 * me:2 * me + 2], T.lst1[:, 14:16]))
+    W("v", k)
+    inv = V(v.tensor_scalar(T.inv[:], T.lf[:], 127.5, 100.0, OP.is_gt, OP.mult))
+    kx = V(v.tensor_tensor(T.idx[:, 0:512:32], T.lf[:], T.idc[:], OP.add))
+    W("v", *ar)
+    qa.append(V(v.quantize_mx(T.aqc[:, 256:512], T.aqs[:, 256:512], T["at"][:, 1024:2048])))
+    hc = [[], []]
+    for h in range(2):
+        for i in range(4):
+            W("t", qv, qa[h], vc[i] if h == 0 else ar[i])
+            o = 2048 * h + 512 * i
+            m = mm(o, 256, "vq", 128 * i, "aq", 256 * h)
+            out = T.ht[:, 1024 * h + i:1024 * h + 1024:4]
+            if i % 2 == 0:
+                W("s", m)
+                hc[h].append(S(sc.activation(out, T.ps[:, o:o + 256], AF.Copy, scale=0.0625)))
+            else:
+                W("v", m)
+                hc[h].append(V(v.tensor_scalar(out, T.ps[:, o:o + 256], 0.0625, None, OP.mult)))
+        W("v", *hc[h])
+        hc[h].append(V(v.quantize_mx(T.hqc[:, 256 * h:256 * h + 256], T.hqs[:, 256 * h:256 * h + 256], T.ht[:, 1024 * h:1024 * h + 1024])))
+    for h in range(2):
+        W("t", hc[h][4], qp2, hc[0][h])
+        m = mm(512 * h, 256, "p2q", 0, "hq", 256 * h)
+        W("v", m)
+        zb = V(v.tensor_scalar(T.bs2[:, 256 * h:256 * h + 256], T.ps[:, 512 * h:512 * h + 256], 0.0, wcol, OP.is_lt, OP.mult))
+        W("v", zb)
+        k = V(v.transpose(T.tr2[:, 256 * h:256 * h + 256], T.bs2[:, 256 * h:256 * h + 256]))
+    W("v", k, inv)
+    V(v.tensor_tensor(T.nx[:], T.tr2[:, 0:512:32], T.inv[:], OP.add))
+    k = V(v.tensor_tensor(T.ny[:], T.tr2[:, 1:512:32], T.tr2[:, 2:512:32], OP.add))
+    W("v", k)
+    k = V(v.tensor_tensor(T.num2[:], T.nx[:], T.ny[:], OP.add))
+    W("v", k)
+    for i in range(8):
+        k = V(v.tensor_scalar(T.e32[:, i:512:32], T.num2[:], float(i - K0), None, OP.is_equal))
+    V(v.tensor_scalar(T.n64[:], T.num2[:], 64.0, 64.0 * K0 - 1.0, OP.mult, OP.add))
+    W("s", k)
+    e8 = S(sc.activation(T.e8[:], T.e32[:].indirect(T.offdb[:, 0:8]), AF.Copy))
+    W("v", k)
+    k = V(v.transpose(T.m2[:], T.e32[:]))
+    W("v", k)
+    k = V(v.tensor_tensor_scan(T.s2[:], T.m2[:], T.m2[:], 0.0, OP.add, OP.max))
+    W("v", k)
+    k = V(v.transpose(T.t2[:], T.s2[:]))
+    W("v", k, e8)
+    k = V(v.tensor_tensor(T.rr[:], T.t2[:].indirect(T.offdb[:, 0:8]), T.e8[:], OP.mult))
+    W("v", k)
+    k = V(v.tensor_tensor(T.ra[:], T.rr[:, 0:64], T.rr[:, 64:128], OP.add))
+    W("v", k)
+    k = V(v.tensor_tensor(T.rb[:], T.ra[:, 0:32], T.ra[:, 32:64], OP.add))
+    W("v", k)
+    k = V(v.tensor_tensor(T.rc[:], T.rb[:, 0:16], T.rb[:, 16:32], OP.add))
+    W("v", k)
+    V(v.tensor_scalar(T.ov[:], T.rc[:], 64.5, 5000.0, OP.is_gt, OP.mult))
+    k = V(v.tensor_tensor(T.su[:], T.rc[:], T.n64[:], OP.add))
+    W("v", k)
+    k = V(v.tensor_tensor(T.sv[:], T.su[:], T.ov[:], OP.add))
+    W("v", k)
+    k = V(v.tensor_tensor(T.sw[:], T.sv[:], T.dump[:], OP.min))
+    W("v", k)
+    k = V(v.tensor_copy(T.sc[:], T.sw[:]))
+    W("v", k)
+    k = V(v.tensor_copy(T.win[:, 16:784].indirect(T.sc[:, 0:16]), T.vals[:]))
+    W("v", k)
+    k = V(v.transpose(T.ta[:], T.win[:, 16:528]))
+    k2 = V(v.transpose(T.tb[:], T.win[:, 0:544]))
+    W("v", k)
+    V(v.tensor_tensor(T.wm[:, 1:33:2], T.ta[:, 0:512:32], T.ta[:, 16:512:32], OP.min))
+    W("v", k2)
+    k = V(v.tensor_tensor(T.wm[:, 0:33:2], T.tb[:, 0:544:32], T.tb[:, 16:544:32], OP.min))
+    W("v", k)
+    V(v.tensor_scalar(T.x2[:], T.wm[:, 0:32], mO, None, OP.mult))
+    k = V(v.tensor_scalar(T.y2[:], T.wm[:, 1:33], mE, None, OP.mult))
+    W("v", k)
+    k = V(v.tensor_tensor(T.z2[:], T.x2[:], T.y2[:], OP.add))
+    W("v", k)
+    of2 = V(v.tensor_scalar(T.offs2[:], T.z2[:], 256.0, None, OP.add))
+    W("v", of2)
+    W("s", of2, *hc[0], *hc[1])
+    c2r = pickc("sl2r", 0, 256, "hq", 514, "offs2", 0, 16)
+    s2r = picks("sl2r", 0, 256, "hq", 514, "offs2", 0, 16)
+    idr = V(v.transpose(T.idrow[:, 0:512], T.idx[:]))
+    c2d = pickc("sl2d", 0, 192, "hq", 514, "offs2", 16, 28)
+    s2d = picks("sl2d", 0, 192, "hq", 514, "offs2", 16, 28)
+    c2o = pickc("hl", own, own + 64, "hq", 514, "offs2", 28, 32)
+    s2o = picks("hl", own, own + 64, "hq", 514, "offs2", 28, 32)
+    W("s", idr)
+    ig = [S(sc.activation(T.idg[:, 256 * h:256 * h + 256], T.idrow[:].indirect(T.offs2[:, 16 * h:16 * h + 16]), AF.Copy)) for h in range(2)]
+    idm = []
+    for h in range(2):
+        W("v", ig[h])
+        k = V(v.transpose(T.idt[:, 256 * h:256 * h + 256], T.idg[:, 256 * h:256 * h + 256]))
+        W("v", k)
+        V(v.tensor_copy(T.idm[0:32, 4 * h:4 * h + 4], T.idt[0:32, 256 * h:256 * h + 256:64]))
+        idm.append(V(v.tensor_copy(T.idm[32:64, 4 * h:4 * h + 4], T.idt[32:64, 256 * h + 32:256 * h + 256:64])))
+    W("g", c2r)
+    fused(far_parts(lambda i: u8("sl2rc", 64 * i, 64 * i + 64), u8("r2c", 0, 64), "rc2"))
+    W("g", s2r)
+    fused(far_parts(lambda i: T.sl2rs[:, 64 * i:64 * i + 64], T.r2s[:, 0:64], "rs2"))
+    W("g", c2d)
+    fused(near_parts(lambda i: u8("sl2dc", 64 * i, 64 * i + 64), u8("hlc", own, own + 64), "a2d"))
+    W("g", s2d)
+    fused(near_parts(lambda i: T.sl2ds[:, 64 * i:64 * i + 64], T.hls[:, own:own + 64], "a2d", True))
+    W("g", idm[0])
+    fused(far_parts(lambda i: T.idm[:, i:i + 1], T.r2l[:, 0:1], "rl2", True))
+    W("g", idm[1])
+    fused(near_parts(lambda i: T.idm[:, 4 + i:5 + i], T.idl[:, me:me + 1], "l2d"))
+
+    def store_oc(d):
+        load("y", "st", T.oc[:, 256 * d:256 * d + 256], u8("hlc", 64 * d, 64 * d + 64))
+
+    def store_id(d):
+        src = T.idm[0:64, 7:8] if d == me else T.idl[0:64, d:d + 1]
+        return load("s", "sts", T["id"][0:1, 64 * d:64 * d + 64], src)
+    W("y", c2o, s2o)
+    store_oc(me)
+    W("y", ("a2d", nd))
+    for d in near:
+        store_oc(d)
+    arr = [("a2d", nd), ("a2r", 2 * nf), c2o, s2o]
+    W("t", qw, *arr)
+    W("t", hc[0][2], hc[0][3])
+    y0 = mm(1024, 256, "wq", 0, "hl", 0)
+    y1 = mm(1536, 256, "wq", 0, "hl", 256)
+    W("s", y0)
+    k0 = S(sc.activation(T.ysb[:, 0:256], T.ps[:, 1024:1280], AF.Copy))
+    W("v", y1)
+    k1 = V(v.tensor_copy(T.ysb[:, 256:512], T.ps[:, 1536:1792]))
+    W("y", *arr)
+    for d in far:
+        store_oc(d)
+    for b in range(4):
+        load("y", "st", T.osc[4 * b:4 * b + 4, 0:512], T.hls[32 * b:32 * b + 4, 0:512])
+    W("y", k0)
+    load("y", "st", T.y[:, 0:256], T.ysb[:, 0:256])
+    W("y", k1)
+    st = load("y", "st", T.y[:, 256:512], T.ysb[:, 256:512])
+    W("s", idm[1], ("l2d", ndl))
+    for d in near + [me]:
+        store_id(d)
+    W("s", ("l2r", nf))
+    for d in far:
+        sts = store_id(d)
+    W("y", st)
+    W("s", sts)
+    W("g", ("ls", lsn[0]), ("pv", cnt["v"]), ("psc", cnt["s"]), ("pt", cnt["t"]), ("pg", cnt["g"]))

@@ -1,5 +1,5 @@
 from concourse.bass import DstId, RemoteDMATransfer
-from concourse.mybir import dt, AluOpType as OP, AxisListType, ActivationFunctionType as AF
+from concourse.mybir import dt, AluOpType as OP, ActivationFunctionType as AF
 
 F8, U8, BF, F32, U16, I32 = "float8_e4m3fn_x4", "uint8", "bfloat16", "float32", "uint16", "int32"
 SCRATCH = {"ps": ("psum", [128, 4096], F32)}
@@ -8,17 +8,24 @@ for _n, _w in (("xq", 130), ("plq", 128), ("p2q", 128), ("wq", 128), ("wvq", 512
                ("r1", 64), ("r2", 64)):
     SCRATCH[_n + "c"] = ("sbuf", [128, _w], F8)
     SCRATCH[_n + "s"] = ("sbuf", [128, _w], U8)
-for _t, _b in ((BF, "xt 520 plt 512 p2t 512 wt 512 wvt 2048 zt 512 vt 2048 at 2048 ht 2048 vals 256 bs1 128 tr1 128 e1 128 m1 128 "
-                    "s1 128 jS 2048 jV 2048 lst1 16 ll1 16 bs2 512 tr2 512 e32 512 e8 128 m2 512 s2 512 t2 512 rr 128 ra 64 rb 32 "
-                    "win 784 ta 512 tb 544 wm 34 r1l 2"),
-               (F32, "cf 4 wc 8 wcol 8 mE 8 i16 16 u16 8 thr 16 addc 8 kc1 128 l32x 8 i8 8 l4x 8 ic 32 p16 8 iv 256 idu 16 dump 16 "
-                     "idc 16 ny1 8 num1 8 x1 32 x1t 32 la 16 lb 16 lf 16 inv 16 idx 512 idrow 520 nx 16 ny 16 num2 16 rc 16 n64 16 "
-                     "ov 16 su 16 sv 16 sw 16 x2 32 y2 32 z2 32 idg 512 idt 512 idm 8 idl 8 ysb 512 r2l 1"),
-               (U16, "rep1 8 offdb 8 offc 32 offs1 32 sc 16 offs2 32"), (I32, "pI 2 ci 4")):
+for _t, _b in ((BF, "xt 520 plt 512 p2t 512 wt 512 wvt 2048 zt 800 vt 2048 at 2048 ht 2048 vals 256 nb1 16 ns1 16 e1 128 m1 128 "
+                    "s1 128 jS 2048 jV 2048 jW 2048 lst1 16 ll1 16 nb2 64 ns2 64 e32 512 m2 512 s2 512 t2 512 rr 128 rs 128 "
+                    "keep4 32 keep8 64 win 784 tt 1056 wm 48 vin 512 vtr 512 r1l 2"),
+               (F32, "cf 8 i16 16 u16 8 thr 16 kc1 128 kc8 64 ic 32 iv 32 iw 32 idu 16 cg 16 tz1 128 tz2 512 "
+                     "x1 32 x1t 32 d0 32 d1 32 sw 32 n64 16 ia 32 ib 16 idf 32 idt 32 ysb 512"),
+               (U16, "rep1 8 rep8 4 offc 32 offs1 32 sc 16 offs2 32 offl 2 offv 16 offf 2 offh 2 idm 16 idl 64 r2l 2"),
+               (I32, "pI 2 ci 8")):
     _b = _b.split()
     for _i in range(0, len(_b), 2):
         SCRATCH[_b[_i]] = ("sbuf", [128, int(_b[_i + 1])], _t)
-SEMAPHORES = ("pv psc pt pg ldx ldpl ldwv ldp2 ldw a1 l1 a2d a2r l2d l2r ls st sts rc1 rs1 rl1 rc2 rs2 rl2").split()
+SEMAPHORES = ("pv psc pt pg ldx ldpl ldwv ldp2 ldw a1 l1 a2 l2 ls st sts rc1 rs1 rl1 rc2 rs2 rl2").split()
+
+ORDER = ("pc0 pp0 pp1 mV00 pc1 mA01 mA00 eA01:v eV00:s mV20 mV30 eA00:v mV10 eV30:v eV20:s mA10 mA20 mA30 eV10:v mA11 sm eA10:s "
+         "eA20:v eA30:s mA21 mA31 qV1 qA0 eA11:s eA31:s eA21:v mO30 qV0 qA1 mO20 mO00 qA2 mO10 eO30:s mO12 mO31 mO11 eO20:s tv "
+         "eO00:s mO01 mO21 mO22 eO12:s eO01:s eO10:v eO21:s eO31:v eO22:s mO32 mO02 eO02:s qH0 eO11:v eO32:v mZ0 qH1 mZ1 eZ0 qH2 "
+         "eZ1 nb0 mZ2 eZ2 ns0 nb1 e0 ns1 m0 e1 s0 m1 t0 s1 rr0 sv t1 sg0 rr1 ov0 sg1 sw0 ov1 sc0 sw1 sca0 sc1 sca1").split()
+PIECES = ((0, 256), (256, 384), (384, 512))
+HALVES = ((0,), (1, 2))
 
 
 def kmap(topo, cores, s):
@@ -65,9 +72,9 @@ def relay_program(g, core, T, topo):
         go("rc1", 4, T.clc[:, a:b].bitcast(dt.uint8), T.r1c[:, 0:64].bitcast(dt.uint8), "a1")
         go("rs1", 4, T.cls[:, a:b], T.r1s[:, 0:64], "a1")
         go("rl1", 2, T.ll1[:, 2 * s:2 * s + 2], T.r1l[:, 0:2], "l1")
-        go("rc2", 4, T.hlc[:, a:b].bitcast(dt.uint8), T.r2c[:, 0:64].bitcast(dt.uint8), "a2r")
-        go("rs2", 4, T.hls[:, a:b], T.r2s[:, 0:64], "a2r")
-        go("rl2", 2, T.idl[:, s:s + 1], T.r2l[:, 0:1], "l2r")
+        go("rc2", 4, T.hlc[:, a:b].bitcast(dt.uint8), T.r2c[:, 0:64].bitcast(dt.uint8), "a2")
+        go("rs2", 4, T.hls[:, a:b], T.r2s[:, 0:64], "a2")
+        go("rl2", 2, T.idl[:, 8 * s:8 * s + 2], T.r2l[:, 0:2], "l2")
         g.wait_ge(T.sem.ls, 6 * len(es))
 
 
@@ -77,8 +84,8 @@ def rank_program(g, core, T, topo):
         return relay_program(g, core, T, topo)
     C = T.cores
     w3, flip, kof, dof, far = kmap(topo, C, me)
-    near = [d for d in range(8) if d != me and d not in far]
     K0 = sum(w3[b] for b in range(3) if flip >> b & 1)
+    ws = [float(-w3[b] if flip >> b & 1 else w3[b]) for b in range(3)]
     rl = relays(topo, C, me)
     Q = {"v": g.vector, "s": g.scalar, "t": g.tensor, "g": g, "y": g.sync}
     SEM = {"v": "pv", "s": "psc", "t": "pt", "g": "pg"}
@@ -110,9 +117,6 @@ def rank_program(g, core, T, topo):
         return (sem, cnt[sem])
     v, sc, te = g.vector, g.scalar, g.tensor
 
-    def C1(k, inst):
-        return V(inst)
-
     ldx = load("y", "ldx", T.xt[:, 0:512], T.x[:])
     ldpl = load("s", "ldpl", T.plt[:, 0:128], T.pl[:, 0:128])
     W("y", ldx)
@@ -122,38 +126,31 @@ def rank_program(g, core, T, topo):
 
     fl = {"allow_small_or_imprecise_dtypes": True}
     gi = done("g", g.iota(T.pI[:, 0:1], [[0, 1]], 0, 1))
-    done("g", g.iota(T.kc1[:], [[0, 4], [1, 8], [0, 4]], -K0, 0, **fl))
-    gi2 = done("g", g.iota(T.i16[:], [[1, 16]], 0, 0, **fl))
-    done("g", g.iota(T.i8[:], [[1, 8]], 0, 0, **fl))
+    done("g", g.iota(T.i16[:], [[1, 16]], 0, 0, **fl))
+    gi2 = done("g", g.iota(T.kc1[:], [[0, 4], [1, 8], [0, 4]], -K0, 0, **fl))
     done("g", g.iota(T.ic[:], [[1, 4], [64, 8]], 0, 0, **fl))
-    done("g", g.iota(T.iv[:], [[32, 16], [1, 16]], -256, 0, **fl))
-    done("g", g.iota(T.idu[:], [[16, 16]], 512, 0, **fl))
-    gi3 = done("g", g.iota(T.idc[:], [[128, 8], [0, 2]], 0, 0, **fl))
+    done("g", g.iota(T.iv[:], [[32, 16], [0, 2]], -256, 0, **fl))
+    done("g", g.iota(T.iw[:], [[128, 8], [0, 4]], 0, 0, **fl))
+    gi3 = done("g", g.iota(T.kc8[:], [[0, 8], [1, 8]], -K0, 0, **fl))
     zx = V(v.memset(T.xt[:, 512:520], 0.0))
+    V(v.memset(T.nb1[:, 0:16:4], 0.0))
     for b in range(4):
-        rep1 = V(v.memset(T.rep1[:, 2 * b:2 * b + 2], b))
+        V(v.memset(T.keep4[:, b:32:4], float(min(b, 1))))
+        rep1 = V(v.memset(T.rep1[:, 2 * b:2 * b + 2], 4 * b + 3))
     W("v", gi)
     V(v.tensor_scalar(T.ci[:, 0:1], T.pI[:, 0:1], 31, None, OP.bitwise_and))
-    V(v.tensor_scalar(T.ci[:, 1:2], T.pI[:, 0:1], 15, None, OP.bitwise_and))
-    V(v.tensor_scalar(T.ci[:, 2:3], T.pI[:, 0:1], 4, 1, OP.arith_shift_right, OP.bitwise_and))
-    c0 = V(v.tensor_scalar(T.ci[:, 3:4], T.pI[:, 0:1], 3, None, OP.bitwise_and))
+    V(v.tensor_scalar(T.ci[:, 1:2], T.pI[:, 0:1], 3, None, OP.bitwise_and))
+    V(v.tensor_scalar(T.ci[:, 2:3], T.pI[:, 0:1], 15, None, OP.bitwise_and))
+    c0 = V(v.tensor_scalar(T.ci[:, 3:4], T.pI[:, 0:1], 4, 1, OP.arith_shift_right, OP.bitwise_and))
     W("v", c0)
-    c0 = V(v.tensor_copy(T.cf[:], T.ci[:]))
+    c0 = V(v.tensor_copy(T.cf[:, 0:4], T.ci[:, 0:4]))
     W("v", c0)
-    lane, l16, mO, u4 = (T.cf[:, i:i + 1] for i in range(4))
-    for b in range(3):
-        c1 = V(v.tensor_scalar(T.wc[:, b:b + 1], lane, float(b), float(-w3[b] if flip >> b & 1 else w3[b]), OP.is_equal, OP.mult))
+    lane, u4, l16, mO, par, b3, l2 = (T.cf[:, i:i + 1] for i in range(7))
     c2 = V(v.tensor_scalar(T.u16[:, 0:1], u4, 16.0, 0.5, OP.mult, OP.add))
-    nS = 9
-    c3 = V(v.tensor_scalar(T.addc[:, 0:1], l16, nS - 0.5, 64.0, OP.is_lt, OP.mult))
-    c4 = V(v.tensor_scalar(T.mE[:, 0:1], mO, -1.0, 1.0, OP.mult, OP.add))
-    W("v", c1)
-    c1 = V(v.tensor_tensor(T.wc[:, 3:4], T.wc[:, 0:1], T.wc[:, 1:2], OP.add))
-    W("v", c1)
-    wc = V(v.tensor_tensor(T.wcol[:, 0:1], T.wc[:, 3:4], T.wc[:, 2:3], OP.add))
+    c3 = V(v.tensor_scalar(T.offl[:, 0:1], l16, 2.0, mO, OP.mult, OP.add))
+    nS = 6
     W("v", c2, gi2)
     thr = V(v.tensor_scalar(T.thr[:], T.i16[:], T.u16[:, 0:1], None, OP.add))
-    wcol, mE = T.wcol[:, 0:1], T.mE[:, 0:1]
 
     W("v", ldpl)
     for a in range(1, 4):
@@ -168,16 +165,15 @@ def rank_program(g, core, T, topo):
                                       T[r + "c"][:, ro:ro + n], T[r + "s"][:, ro:ro + n], True, True))
     W("t", qpl, qx)
     z = mm(0, 128, "plq", 0, "xq", 0)
-    W("v", z, wc)
-    z1 = V(v.tensor_scalar(T.bs1[:], T.ps[:, 0:128], 0.0, wcol, OP.is_lt, OP.mult))
+    W("v", z, rep1)
+    z1 = V(v.transpose(T.tz1[:], T.ps[:, 0:128]))
     W("v", z1)
-    k = V(v.transpose(T.tr1[:], T.bs1[:]))
+    for b in range(3):
+        k = V(v.tensor_scalar(T.nb1[:, b + 1:16:4], T.tz1[:, b:128:32], 0.0, ws[b], OP.is_lt, OP.mult))
     W("v", k)
-    k = V(v.tensor_tensor(T.ny1[:, 0:4], T.tr1[:, 1:128:32], T.tr1[:, 2:128:32], OP.add))
-    W("v", k)
-    k = V(v.tensor_tensor(T.num1[:, 0:4], T.tr1[:, 0:128:32], T.ny1[:, 0:4], OP.add))
-    W("v", k, rep1, gi2)
-    k = V(v.tensor_tensor(T.e1[:], T.num1[:, 0:4].indirect(T.rep1[:, 0:8]), T.kc1[:], OP.is_equal))
+    k = V(v.tensor_tensor_scan(T.ns1[:], T.keep4[:, 0:16], T.nb1[:], 0.0, OP.mult, OP.add))
+    W("v", k, gi2)
+    k = V(v.tensor_tensor(T.e1[:], T.ns1[:, 0:16].indirect(T.rep1[:, 0:8]), T.kc1[:], OP.is_equal))
     W("v", k)
     k = V(v.transpose(T.m1[:], T.e1[:]))
     W("v", k)
@@ -186,16 +182,20 @@ def rank_program(g, core, T, topo):
     W("v", k, thr)
     for i in range(nS):
         ks = S(sc.activation(T.jS[:, 128 * i:128 * i + 128], T.s1[:], AF.Sign, bias=T.thr[:, i:i + 1], scale=-1.0, accum_out=T.x1[:, i:i + 1]))
-    cs = [V(v.tensor_scalar(T.jV[:, 128 * i:128 * i + 128], T.s1[:], T.thr[:, i:i + 1], 2.0, OP.is_lt, OP.mult)) for i in range(nS, 16)]
+    nV = 128 * (16 - nS)
     for i in range(nS, 16):
-        W("v", cs[i - nS])
-        k = V(v.tensor_reduce(T.x1[:, i:i + 1], T.jV[:, 128 * i:128 * i + 128], AxisListType.X, OP.add))
-    W("v", k, ks)
-    k = V(v.tensor_copy(T.x1[:, 16:32], T.x1[:, 0:16]))
+        k = V(v.tensor_scalar(T.jV[:, 128 * (i - nS):128 * (i - nS) + 128], T.s1[:], T.thr[:, i:i + 1], None, OP.is_gt))
+    W("v", k)
+    k = V(v.tensor_tensor_scan(T.jW[:, 0:nV], T.jV[:, 0:nV], T.jV[:, 0:nV], 0.0, OP.mult, OP.add))
+    W("v", k)
+    for a in (0, 16):
+        V(v.tensor_scalar(T.x1[:, a + nS:a + 16], T.jW[:, 127:nV:128], -2.0, 128.0, OP.mult, OP.add))
+    W("v", ks)
+    k = V(v.tensor_copy(T.x1[:, 16:16 + nS], T.x1[:, 0:nS]))
     W("v", k)
     k = V(v.transpose(T.x1t[:], T.x1[:]))
     W("v", k, c3)
-    of1 = V(v.tensor_scalar(T.offs1[:], T.x1t[:], 0.5, T.addc[:, 0:1], OP.mult, OP.add))
+    of1 = V(v.tensor_scalar(T.offs1[:], T.x1t[:], 0.5, 64.0, OP.mult, OP.add))
     W("v", of1)
     W("s", of1)
 
@@ -211,11 +211,7 @@ def rank_program(g, core, T, topo):
     s1d = picks("sl1d", 0, 192, "xq", 130, "offs1", 16, 28)
     c1o = pickc("cl", own, own + 64, "xq", 130, "offs1", 28, 32)
     s1o = picks("cl", own, own + 64, "xq", 130, "offs1", 28, 32)
-    W("v", c4)
-    V(v.tensor_scalar(T.la[:], T.offs1[:, 0:32:2], mE, None, OP.mult))
-    k = V(v.tensor_scalar(T.lb[:], T.offs1[:, 1:32:2], mO, None, OP.mult))
-    W("v", k)
-    l1 = V(v.tensor_tensor(T.lst1[:], T.la[:], T.lb[:], OP.add))
+    l1 = V(v.tensor_scalar(T.lst1[:], T.x1t[:, 0:32].indirect(T.offl[:, 0:1]), 0.5, 64.0, OP.mult, OP.add))
 
     lsn = [0]
 
@@ -249,25 +245,42 @@ def rank_program(g, core, T, topo):
     fused(near_parts(lambda i: T.lst1[:, 8 + 2 * i:10 + 2 * i], T.ll1[:, 2 * me:2 * me + 2], "l1"))
 
     W("v", gi3, c0)
-    V(v.tensor_scalar(T.l32x[:, 0:1], l16, 32.0, None, OP.mult))
-    V(v.tensor_scalar(T.p16[:, 0:1], mO, 16.0, None, OP.mult))
-    k = V(v.tensor_scalar(T.l4x[:, 0:1], l16, 4.0, None, OP.mult))
+    V(v.tensor_scalar(T.ci[:, 4:5], T.pI[:, 0:1], 1, None, OP.bitwise_and))
+    V(v.tensor_scalar(T.ci[:, 5:6], T.pI[:, 0:1], 3, 1, OP.arith_shift_right, OP.bitwise_and))
+    V(v.tensor_scalar(T.ci[:, 6:7], T.pI[:, 0:1], 1, 7, OP.arith_shift_right, OP.bitwise_and))
+    V(v.memset(T.vin[:], 0.0))
+    k = V(v.memset(T.zt[:], 0.0))
     W("v", k)
-    oc_ = V(v.tensor_scalar(T.offc[:], T.ic[:], T.l4x[:, 0:1], None, OP.add))
+    V(v.tensor_copy(T.cf[:, 4:7], T.ci[:, 4:7]))
+    V(v.tensor_scalar(T.cg[:, 0:1], l16, 4.0, None, OP.mult))
+    V(v.tensor_scalar(T.cg[:, 1:2], l16, 0.0, 256.0, OP.is_equal, OP.mult))
+    V(v.tensor_scalar(T.cg[:, 2:3], mO, -33.0, 17.0, OP.mult, OP.add))
+    k = V(v.tensor_scalar(T.cg[:, 3:4], mO, 16.0, None, OP.mult))
+    W("v", k)
+    W("s", k)
+    wi = S(sc.activation(T.win[:], T.zt[:, 0:784], AF.Identity, bias=T.cg[:, 1:2]))
+    oc_ = V(v.tensor_scalar(T.offc[:], T.ic[:], T.cg[:, 0:1], None, OP.add))
+    V(v.tensor_scalar(T.cg[:, 4:5], b3, 4.0, 3.0, OP.mult, OP.add))
+    V(v.tensor_scalar(T.cg[:, 5:6], par, T.cg[:, 2:3], T.cg[:, 3:4], OP.mult, OP.add))
     W("v", ldwv)
     qwv = V(v.quantize_mx(T.wvqc[:, 0:512], T.wvqs[:, 0:512], T.wvt[:, 0:2048]))
-    V(v.tensor_scalar(T.offdb[:], T.i8[:], T.l32x[:, 0:1], None, OP.add))
-    V(v.tensor_scalar(T.vals[:], T.iv[:], T.p16[:, 0:1], None, OP.add))
-    V(v.tensor_scalar(T.dump[:], T.idu[:], l16, None, OP.add))
-    V(v.memset(T.win[:], 256.0))
+    W("v", qwv)
+    V(v.tensor_scalar(T.rep8[:], T.i16[:, 0:4], 8.0, T.cg[:, 4:5], OP.mult, OP.add))
+    V(v.tensor_scalar(T.offh[:], T.i16[:, 0:2], 8.0, l2, OP.mult, OP.add))
+    V(v.tensor_scalar(T.offv[:], T.i16[:], 32.0, lane, OP.mult, OP.add))
+    V(v.tensor_scalar(T.vin[:, 0:512:16], T.iv[:], lane, None, OP.add))
+    V(v.tensor_copy(T.vin[:, 2:512:16], T.iw[:]))
+    V(v.tensor_scalar(T.keep8[:], T.kc8[:], 0.5 - K0, None, OP.is_gt))
+    V(v.memset(T.d0[:, 0:32:2], 1000000.0))
     V(v.memset(T.e32[:], 0.0))
-    V(v.memset(T.idx[:], 0.0))
-    V(v.memset(T.idrow[:, 512:520], -1.0))
-    V(v.memset(T.idm[:], 0.0))
-    W("v", ldp2)
+    V(v.memset(T.idf[:, 16:32], 0.0))
+    V(v.tensor_scalar(T.idu[:], T.i16[:], 16.0, 512.0, OP.mult, OP.add))
+    k = V(v.tensor_tensor(T.cg[:, 6:7], T.cg[:, 5:6], l2, OP.add))
+    W("v", k, ldp2)
+    V(v.tensor_scalar(T.offf[:], T.i16[:, 0:2], 8.0, T.cg[:, 6:7], OP.mult, OP.add))
+    V(v.tensor_scalar(T.d1[:, 1:32:2], T.idu[:], l16, None, OP.add))
     for a in range(1, 4):
-        V(v.tensor_copy(T.p2t[:, 128 * a:128 * a + 128], T.p2t[:, 0:128]))
-    k = V(v.memset(T.zt[:], 0.0))
+        k = V(v.tensor_copy(T.p2t[:, 128 * a:128 * a + 128], T.p2t[:, 0:128]))
     W("v", k, ldw)
     V(v.quantize_mx(T.hqc[:, 512:640], T.hqs[:, 512:640], T.zt[:, 0:512]))
     qp2 = V(v.quantize_mx(T.p2qc[:, 0:128], T.p2qs[:, 0:128], T.p2t[:, 0:512]))
@@ -281,179 +294,167 @@ def rank_program(g, core, T, topo):
             ndl += len(near_engines(topo, C, s, me))
             nd += len(near_engines(topo, C, s, me)) + len(near_engines(topo, C, s, me, True))
     a1 = ("a1", nd + 2 * nf)
-    W("v", a1, c1o, s1o, oc_)
-    W("s", a1, c1o, s1o, oc_)
-    W("t", a1, c1o, s1o, qwv)
-    pc, pp = [], []
-    for t in range(4):
-        pc.append(pickc("cp", 128 * t, 128 * t + 128, "cl", 512, "offc", 8 * t, 8 * t + 8))
-        pp.append(picks("cp", 128 * t, 128 * t + 128, "cl", 512, "offc", 8 * t, 8 * t + 8))
-    vc, al, ar = [], [], []
-    for t in range(4):
-        W("t", pc[t], pp[t], z1)
-        m = mm(512 * t, 512, "cp", 128 * t, "wvq", 0)
-        W("v", m)
-        vc.append(V(v.tensor_copy(T.vt[:, t:2048:4], T.ps[:, 512 * t:512 * t + 512])))
-    for h, acc in ((0, al), (1, ar)):
-        for t in range(4):
-            if h:
-                W("t", al[t])
-            m = mm(2048 + 512 * t, 256, "cp", 128 * t, "cl", 256 * h)
-            W("s", m)
-            acc.append(S(sc.activation(T["at"][:, 1024 * h + t:1024 * h + 1024:4], T.ps[:, 2048 + 512 * t:2304 + 512 * t], AF.Relu, scale=0.0625)))
-    W("v", *vc)
-    qv = V(v.quantize_mx(T.vqc[:, 0:512], T.vqs[:, 0:512], T.vt[:, 0:2048]))
-    W("v", *al)
-    qa = [V(v.quantize_mx(T.aqc[:, 0:256], T.aqs[:, 0:256], T["at"][:, 0:1024]))]
-    W("v", ("l1", ndl + nf), l1)
-    if me > 0:
-        V(v.tensor_copy(T.lf[:, 0:2 * me], T.ll1[:, 0:2 * me]))
-    if me < 7:
-        V(v.tensor_copy(T.lf[:, 2 * me + 2:16], T.ll1[:, 2 * me + 2:16]))
-    k = V(v.tensor_copy(T.lf[:, 2 * me:2 * me + 2], T.lst1[:, 14:16]))
+    W("v", a1, c1o, s1o, qw)
+    W("s", a1, c1o, s1o, qw)
+    W("t", a1, c1o, s1o, qw)
+    D, bank, users = {}, {}, [z1] + [None] * 7
+
+    def product(x, n, l, lo, r, ro, *deps):
+        b = len(bank) % 8
+        W("t", *(list(deps) + ([users[b]] if users[b] else [])))
+        bank[x] = b
+        return mm(512 * b, n, l, lo, r, ro)
+
+    def leave(x, q, out, n, func, scale):
+        src = T.ps[:, 512 * bank[x]:512 * bank[x] + n]
+        W(q, D["m" + x])
+        if q == "s":
+            k = S(sc.activation(out, src, func, scale=scale))
+        elif func == AF.Relu:
+            k = V(v.tensor_scalar(out, src, 0.0, scale, OP.max, OP.mult))
+        else:
+            k = V(v.tensor_copy(out, src) if scale == 1.0 else v.tensor_scalar(out, src, scale, None, OP.mult))
+        users[bank[x]] = k
+        return k
+
+    def quant(n, t, a, b, *deps):
+        W("v", *deps)
+        return V(v.quantize_mx(T[n + "c"][:, a:b], T[n + "s"][:, a:b], T[t][:, 4 * a:4 * b]))
+
+    for x in ORDER:
+        x, q = (x + ":").split(":")[:2]
+        j = int(x[-1]) if x[-1] in "0123" else 0
+        a, b = PIECES[j]
+        p0, p1 = 256 * j, 256 * j + 256
+        if x[:2] in ("pc", "pp"):
+            D[x] = (pickc if x[1] == "c" else picks)("cp", 128 * j, 128 + 384 * j, "cl", 512, "offc", 8 * j, 8 + 24 * j)
+        elif x[:2] in ("mV", "mA"):
+            t = int(x[2])
+            D[x] = product(x[1:], 512 if x[1] == "V" else 256, "cp", 128 * t, "wvq" if x[1] == "V" else "cl", p0,
+                           D["pc%d" % min(t, 1)], D["pp%d" % min(t, 1)])
+        elif x[:2] == "eV":
+            D[x] = leave(x[1:], q, T.vt[:, int(x[2]):2048:4], 512, AF.Copy, 1.0)
+        elif x[:2] == "eA":
+            D[x] = leave(x[1:], q, T["at"][:, 4 * p0 + int(x[2]):4 * p1:4], 256, AF.Relu, 0.0625)
+        elif x[:2] == "qV":
+            D[x] = quant("vq", "vt", p0, p1, *[D["eV%d0" % t] for t in range(4)])
+        elif x[:2] == "qA":
+            D[x] = quant("aq", "at", a, b, *[D["eA%d%d" % (t, a // 256)] for t in range(4)])
+        elif x[:2] == "mO":
+            D[x] = product(x[1:], b - a, "vq", 128 * int(x[2]), "aq", a, D["qA%d" % j], D["qV%d" % (int(x[2]) // 2)])
+        elif x[:2] == "eO":
+            D[x] = leave(x[1:], q, T.ht[:, 4 * a + int(x[2]):4 * b:4], b - a, AF.Copy, 0.0625)
+        elif x[:2] == "qH":
+            D[x] = quant("hq", "ht", a, b, *[D["eO%d%d" % (i, j)] for i in range(4)])
+        elif x[:2] == "mZ":
+            D[x] = product(x[1:], b - a, "p2q", 0, "hq", a, D["qH%d" % j])
+        elif x[:2] == "eZ":
+            W("v", D["m" + x[1:]])
+            D[x] = users[bank[x[1:]]] = V(v.transpose(T.tz2[:, a:b], T.ps[:, 512 * bank[x[1:]]:512 * bank[x[1:]] + b - a]))
+        elif x == "sm":
+            W("s", ("l1", ndl + nf), l1)
+            k = S(sc.activation(T.ll1[:, 2 * me:2 * me + 2], T.lst1[:, 14:16], AF.Copy))
+            W("s", k)
+            S(sc.activation(T.vin[:, 1:512:16], T.ll1[:, 0:16].indirect(T.offh[:, 0:2]), AF.Identity, bias=1.0))
+            D[x] = S(sc.activation(T.nb2[:, 0:64:4], T.ll1[:], AF.Relu, bias=-12700.0, scale=100.0))
+        elif x == "tv":
+            W("v", D["sm"])
+            D[x] = V(v.transpose(T.vtr[:], T.vin[:]))
+        elif x == "sv":
+            W("s", D["tv"])
+            D[x] = S(sc.activation(T.vals[:], T.vtr[:, 0:512].indirect(T.offv[:, 0:16]), AF.Copy))
+        elif x[:2] == "nb":
+            W("v", D["sm"], *[D["eZ%d" % h] for h in HALVES[j]])
+            for i in range(3):
+                D[x] = V(v.tensor_scalar(T.nb2[:, 32 * j + 1 + i:32 * j + 32:4], T.tz2[:, p0 + i:p1:32], 0.0, ws[i], OP.is_lt, OP.mult))
+        elif x[:2] == "ns":
+            W("v", D["nb%d" % j])
+            D[x] = V(v.tensor_tensor_scan(T.ns2[:, 32 * j:32 * j + 32], T.keep4[:], T.nb2[:, 32 * j:32 * j + 32], 0.0, OP.mult, OP.add))
+        elif x[:2] == "rr":
+            W("v", D["t%d" % j])
+            V(v.tensor_scalar(T.n64[:, 8 * j:8 * j + 8], T.ns2[:, 32 * j + 3:32 * j + 32:4], 64.0, 64.0 * K0 - 1.0, OP.mult, OP.add))
+            D[x] = V(v.tensor_tensor(T.rr[:, 64 * j:64 * j + 64], T.t2[:, p0:p1:4], T.e32[:, p0:p1:4], OP.mult))
+        elif x[:2] == "sg":
+            W("v", D["rr%d" % j])
+            D[x] = V(v.tensor_tensor_scan(T.rs[:, 64 * j:64 * j + 64], T.keep8[:], T.rr[:, 64 * j:64 * j + 64], 0.0, OP.mult, OP.add))
+        elif x[:2] == "ov":
+            W("v", D["sg%d" % j])
+            r = T.rs[:, 64 * j + 7:64 * j + 64:8]
+            V(v.tensor_scalar(T.d0[:, 16 * j + 1:16 * j + 16:2], r, 64.5, 5000.0, OP.is_gt, OP.mult))
+            D[x] = V(v.tensor_tensor(T.d1[:, 16 * j:16 * j + 16:2], r, T.n64[:, 8 * j:8 * j + 8], OP.add))
+        elif x[:2] == "sw":
+            W("v", D["ov%d" % j])
+            D[x] = V(v.tensor_tensor_scan(T.sw[:, 16 * j:16 * j + 16], T.d0[:, 16 * j:16 * j + 16], T.d1[:, 16 * j:16 * j + 16], 0.0, OP.add, OP.min))
+        elif x[:3] == "sca":
+            W("v", D["sc%d" % j], D["sv"], wi, *([D["sca0"]] if j else []))
+            D[x] = V(v.tensor_copy(T.win[:, 16:784].indirect(T.sc[:, 8 * j:8 * j + 8]), T.vals[:, 128 * j:128 * j + 128]))
+        elif x[:2] == "sc":
+            W("v", D["sw%d" % j])
+            D[x] = V(v.tensor_copy(T.sc[:, 8 * j:8 * j + 8], T.sw[:, 16 * j + 1:16 * j + 16:2]))
+        elif x[0] == "e":
+            W("v", D["ns%d" % j])
+            D[x] = V(v.tensor_tensor(T.e32[:, p0:p1:4], T.ns2[:, 32 * j:32 * j + 32].indirect(T.rep8[:, 0:4]), T.kc8[:], OP.is_equal))
+        elif x[0] == "m":
+            W("v", D["e%d" % j])
+            D[x] = V(v.transpose(T.m2[:, p0:p1], T.e32[:, p0:p1]))
+        elif x[0] == "s":
+            W("v", D["m%d" % j], *([D["s0"]] if j else []))
+            D[x] = V(v.tensor_tensor_scan(T.s2[:, p0:p1], T.m2[:, p0:p1], T.m2[:, p0:p1], T.s2[:, 255:256] if j else 0.0, OP.add, OP.max))
+        else:
+            W("v", D["s%d" % j])
+            D[x] = V(v.transpose(T.t2[:, p0:p1], T.s2[:, p0:p1]))
+    W("v", D["sca1"])
+    V(v.transpose(T.tt[:, 0:512], T.win[:, 16:528]))
+    k = V(v.transpose(T.tt[:, 512:1056], T.win[:, 0:544]))
     W("v", k)
-    inv = V(v.tensor_scalar(T.inv[:], T.lf[:], 127.5, 100.0, OP.is_gt, OP.mult))
-    kx = V(v.tensor_tensor(T.idx[:, 0:512:32], T.lf[:], T.idc[:], OP.add))
-    W("v", *ar)
-    qa.append(V(v.quantize_mx(T.aqc[:, 256:512], T.aqs[:, 256:512], T["at"][:, 1024:2048])))
-    hc = [[], []]
-    for h in range(2):
-        for i in range(4):
-            W("t", qv, qa[h], vc[i] if h == 0 else ar[i])
-            o = 2048 * h + 512 * i
-            m = mm(o, 256, "vq", 128 * i, "aq", 256 * h)
-            out = T.ht[:, 1024 * h + i:1024 * h + 1024:4]
-            if i % 2 == 0:
-                W("s", m)
-                hc[h].append(S(sc.activation(out, T.ps[:, o:o + 256], AF.Copy, scale=0.0625)))
-            else:
-                W("v", m)
-                hc[h].append(V(v.tensor_scalar(out, T.ps[:, o:o + 256], 0.0625, None, OP.mult)))
-        W("v", *hc[h])
-        hc[h].append(V(v.quantize_mx(T.hqc[:, 256 * h:256 * h + 256], T.hqs[:, 256 * h:256 * h + 256], T.ht[:, 1024 * h:1024 * h + 1024])))
-    for h in range(2):
-        W("t", hc[h][4], qp2, hc[0][h])
-        m = mm(512 * h, 256, "p2q", 0, "hq", 256 * h)
-        W("v", m)
-        zb = V(v.tensor_scalar(T.bs2[:, 256 * h:256 * h + 256], T.ps[:, 512 * h:512 * h + 256], 0.0, wcol, OP.is_lt, OP.mult))
-        W("v", zb)
-        k = V(v.transpose(T.tr2[:, 256 * h:256 * h + 256], T.bs2[:, 256 * h:256 * h + 256]))
-    W("v", k, inv)
-    V(v.tensor_tensor(T.nx[:], T.tr2[:, 0:512:32], T.inv[:], OP.add))
-    k = V(v.tensor_tensor(T.ny[:], T.tr2[:, 1:512:32], T.tr2[:, 2:512:32], OP.add))
+    k = V(v.tensor_tensor(T.wm[:, 0:33], T.tt[:, 0:1056:32], T.tt[:, 16:1056:32], OP.min))
     W("v", k)
-    k = V(v.tensor_tensor(T.num2[:], T.nx[:], T.ny[:], OP.add))
-    W("v", k)
-    for i in range(8):
-        k = V(v.tensor_scalar(T.e32[:, i:512:32], T.num2[:], float(i - K0), None, OP.is_equal))
-    V(v.tensor_scalar(T.n64[:], T.num2[:], 64.0, 64.0 * K0 - 1.0, OP.mult, OP.add))
-    W("s", k)
-    e8 = S(sc.activation(T.e8[:], T.e32[:].indirect(T.offdb[:, 0:8]), AF.Copy))
-    W("v", k)
-    k = V(v.transpose(T.m2[:], T.e32[:]))
-    W("v", k)
-    k = V(v.tensor_tensor_scan(T.s2[:], T.m2[:], T.m2[:], 0.0, OP.add, OP.max))
-    W("v", k)
-    k = V(v.transpose(T.t2[:], T.s2[:]))
-    W("v", k, e8)
-    k = V(v.tensor_tensor(T.rr[:], T.t2[:].indirect(T.offdb[:, 0:8]), T.e8[:], OP.mult))
-    W("v", k)
-    k = V(v.tensor_tensor(T.ra[:], T.rr[:, 0:64], T.rr[:, 64:128], OP.add))
-    W("v", k)
-    k = V(v.tensor_tensor(T.rb[:], T.ra[:, 0:32], T.ra[:, 32:64], OP.add))
-    W("v", k)
-    k = V(v.tensor_tensor(T.rc[:], T.rb[:, 0:16], T.rb[:, 16:32], OP.add))
-    W("v", k)
-    V(v.tensor_scalar(T.ov[:], T.rc[:], 64.5, 5000.0, OP.is_gt, OP.mult))
-    k = V(v.tensor_tensor(T.su[:], T.rc[:], T.n64[:], OP.add))
-    W("v", k)
-    k = V(v.tensor_tensor(T.sv[:], T.su[:], T.ov[:], OP.add))
-    W("v", k)
-    k = V(v.tensor_tensor(T.sw[:], T.sv[:], T.dump[:], OP.min))
-    W("v", k)
-    k = V(v.tensor_copy(T.sc[:], T.sw[:]))
-    W("v", k)
-    k = V(v.tensor_copy(T.win[:, 16:784].indirect(T.sc[:, 0:16]), T.vals[:]))
-    W("v", k)
-    k = V(v.transpose(T.ta[:], T.win[:, 16:528]))
-    k2 = V(v.transpose(T.tb[:], T.win[:, 0:544]))
-    W("v", k)
-    V(v.tensor_tensor(T.wm[:, 1:33:2], T.ta[:, 0:512:32], T.ta[:, 16:512:32], OP.min))
-    W("v", k2)
-    k = V(v.tensor_tensor(T.wm[:, 0:33:2], T.tb[:, 0:544:32], T.tb[:, 16:544:32], OP.min))
-    W("v", k)
-    V(v.tensor_scalar(T.x2[:], T.wm[:, 0:32], mO, None, OP.mult))
-    k = V(v.tensor_scalar(T.y2[:], T.wm[:, 1:33], mE, None, OP.mult))
-    W("v", k)
-    k = V(v.tensor_tensor(T.z2[:], T.x2[:], T.y2[:], OP.add))
-    W("v", k)
-    of2 = V(v.tensor_scalar(T.offs2[:], T.z2[:], 256.0, None, OP.add))
+    of2 = V(v.tensor_scalar(T.offs2[:], T.wm[:, 0:33].indirect(T.offf[:, 0:2]), 256.0, None, OP.add))
     W("v", of2)
-    W("s", of2, *hc[0], *hc[1])
+    W("s", of2)
     c2r = pickc("sl2r", 0, 256, "hq", 514, "offs2", 0, 16)
     s2r = picks("sl2r", 0, 256, "hq", 514, "offs2", 0, 16)
-    idr = V(v.transpose(T.idrow[:, 0:512], T.idx[:]))
     c2d = pickc("sl2d", 0, 192, "hq", 514, "offs2", 16, 28)
     s2d = picks("sl2d", 0, 192, "hq", 514, "offs2", 16, 28)
+    k = V(v.tensor_tensor(T.ia[:], T.tt[:, 1:512:16], T.tt[:, 2:512:16], OP.add))
     c2o = pickc("hl", own, own + 64, "hq", 514, "offs2", 28, 32)
     s2o = picks("hl", own, own + 64, "hq", 514, "offs2", 28, 32)
-    W("s", idr)
-    ig = [S(sc.activation(T.idg[:, 256 * h:256 * h + 256], T.idrow[:].indirect(T.offs2[:, 16 * h:16 * h + 16]), AF.Copy)) for h in range(2)]
-    idm = []
-    for h in range(2):
-        W("v", ig[h])
-        k = V(v.transpose(T.idt[:, 256 * h:256 * h + 256], T.idg[:, 256 * h:256 * h + 256]))
-        W("v", k)
-        V(v.tensor_copy(T.idm[0:32, 4 * h:4 * h + 4], T.idt[0:32, 256 * h:256 * h + 256:64]))
-        idm.append(V(v.tensor_copy(T.idm[32:64, 4 * h:4 * h + 4], T.idt[32:64, 256 * h + 32:256 * h + 256:64])))
+    W("v", k)
+    k = V(v.tensor_tensor(T.ib[:], T.ia[:, 0:32:2], T.ia[:, 1:32:2], OP.add))
+    W("v", k)
+    idm = V(v.tensor_copy(T.idm[:], T.ib[:]))
+    ido = V(v.tensor_copy(T.idl[:, 8 * me:8 * me + 2], T.ib[:, 14:16]))
     W("g", c2r)
     fused(far_parts(lambda i: u8("sl2rc", 64 * i, 64 * i + 64), u8("r2c", 0, 64), "rc2"))
     W("g", s2r)
     fused(far_parts(lambda i: T.sl2rs[:, 64 * i:64 * i + 64], T.r2s[:, 0:64], "rs2"))
     W("g", c2d)
-    fused(near_parts(lambda i: u8("sl2dc", 64 * i, 64 * i + 64), u8("hlc", own, own + 64), "a2d"))
+    fused(near_parts(lambda i: u8("sl2dc", 64 * i, 64 * i + 64), u8("hlc", own, own + 64), "a2"))
     W("g", s2d)
-    fused(near_parts(lambda i: T.sl2ds[:, 64 * i:64 * i + 64], T.hls[:, own:own + 64], "a2d", True))
-    W("g", idm[0])
-    fused(far_parts(lambda i: T.idm[:, i:i + 1], T.r2l[:, 0:1], "rl2", True))
-    W("g", idm[1])
-    fused(near_parts(lambda i: T.idm[:, 4 + i:5 + i], T.idl[:, me:me + 1], "l2d"))
+    fused(near_parts(lambda i: T.sl2ds[:, 64 * i:64 * i + 64], T.hls[:, own:own + 64], "a2", True))
+    W("g", idm)
+    fused(far_parts(lambda i: T.idm[:, 2 * i:2 * i + 2], T.r2l[:, 0:2], "rl2", True))
+    fused(near_parts(lambda i: T.idm[:, 8 + 2 * i:10 + 2 * i], T.idl[:, 8 * me:8 * me + 2], "l2"))
 
-    def store_oc(d):
-        load("y", "st", T.oc[:, 256 * d:256 * d + 256], u8("hlc", 64 * d, 64 * d + 64))
-
-    def store_id(d):
-        src = T.idm[0:64, 7:8] if d == me else T.idl[0:64, d:d + 1]
-        return load("s", "sts", T["id"][0:1, 64 * d:64 * d + 64], src)
-    W("y", c2o, s2o)
-    store_oc(me)
-    W("y", ("a2d", nd))
-    for d in near:
-        store_oc(d)
-    arr = [("a2d", nd), ("a2r", 2 * nf), c2o, s2o]
-    W("t", qw, *arr)
-    W("t", hc[0][2], hc[0][3])
-    y0 = mm(1024, 256, "wq", 0, "hl", 0)
-    y1 = mm(1536, 256, "wq", 0, "hl", 256)
-    W("s", y0)
-    k0 = S(sc.activation(T.ysb[:, 0:256], T.ps[:, 1024:1280], AF.Copy))
-    W("v", y1)
-    k1 = V(v.tensor_copy(T.ysb[:, 256:512], T.ps[:, 1536:1792]))
+    arr = [("a2", nd + 2 * nf), c2o, s2o]
+    D["mY0"] = product("Y0", 256, "wq", 0, "hl", 0, *arr)
+    D["mY1"] = product("Y1", 256, "wq", 0, "hl", 256)
     W("y", *arr)
-    for d in far:
-        store_oc(d)
+    load("y", "st", T.oc[:, 0:2048], u8("hlc", 0, 512))
+    W("s", *arr)
     for b in range(4):
-        load("y", "st", T.osc[4 * b:4 * b + 4, 0:512], T.hls[32 * b:32 * b + 4, 0:512])
-    W("y", k0)
-    load("y", "st", T.y[:, 0:256], T.ysb[:, 0:256])
-    W("y", k1)
-    st = load("y", "st", T.y[:, 256:512], T.ysb[:, 256:512])
-    W("s", idm[1], ("l2d", ndl))
-    for d in near + [me]:
-        store_id(d)
-    W("s", ("l2r", nf))
-    for d in far:
-        sts = store_id(d)
+        load("s", "sts", T.osc[4 * b:4 * b + 4, 0:512], T.hls[32 * b:32 * b + 4, 0:512])
+    k0 = leave("Y0", "s", T.ysb[:, 0:256], 256, AF.Copy, 1.0)
+    k1 = leave("Y1", "v", T.ysb[:, 256:512], 256, AF.Copy, 1.0)
+    W("y", k0, k1)
+    st = load("y", "st", T.y[:], T.ysb[:])
+    W("v", ("l2", ndl + nf), ido)
+    for h in range(2):
+        k = V(v.tensor_scalar(T.idf[:, h:16:2], T.idl[:, h:64:8], -1.0, None, OP.add))
+    W("v", k)
+    k = V(v.transpose(T.idt[:], T.idf[:]))
+    W("s", k)
+    sts = load("s", "sts", T["id"][0:1, 0:512], T.idt[0:16, 0:32])
     W("y", st)
     W("s", sts)
     W("g", ("ls", lsn[0]), ("pv", cnt["v"]), ("psc", cnt["s"]), ("pt", cnt["t"]), ("pg", cnt["g"]))

@@ -3,29 +3,28 @@ from concourse.mybir import dt, AluOpType as OP, ActivationFunctionType as AF
 
 F8, U8, BF, F32, U16, I32 = "float8_e4m3fn_x4", "uint8", "bfloat16", "float32", "uint16", "int32"
 SCRATCH = {"ps": ("psum", [128, 4096], F32)}
-for _n, _w in (("xq", 130), ("plq", 128), ("p2q", 128), ("wq", 128), ("wvq", 512), ("sl1r", 256), ("sl1d", 192), ("cl", 512),
-               ("cp", 512), ("vq", 512), ("aq", 512), ("hq", 640), ("sl2r", 256), ("sl2d", 192), ("hl", 512),
-               ("r1", 64), ("r2", 64)):
+for _n, _w in (("xq", 130), ("plq", 128), ("plp", 128), ("p2q", 128), ("p2p", 128), ("wq", 128), ("wvq", 512), ("sl1r", 256),
+               ("sl1d", 128), ("cl", 512), ("cp", 512), ("vq", 512), ("aq", 512), ("hq", 640), ("sl2r", 256), ("sl2d", 192),
+               ("hl", 512), ("xl", 256), ("r0", 32), ("r1", 64), ("r2", 128)):
     SCRATCH[_n + "c"] = ("sbuf", [128, _w], F8)
     SCRATCH[_n + "s"] = ("sbuf", [128, _w], U8)
-for _t, _b in ((BF, "xt 520 plt 512 p2t 512 wt 512 wvt 2048 zt 800 vt 2048 at 2048 ht 2048 vals 256 nb1 16 ns1 16 e1 128 m1 128 "
-                    "s1 128 jS 2048 jV 2048 jW 2048 lst1 16 ll1 16 nb2 64 ns2 64 e32 512 m2 512 s2 512 t2 512 rr 128 rs 128 "
-                    "keep4 32 keep8 64 win 784 tt 1056 wm 48 vin 512 vtr 512 r1l 2"),
-               (F32, "cf 8 i16 16 u16 8 thr 16 kc1 128 kc8 64 ic 32 iv 32 iw 32 idu 16 cg 16 tz1 128 tz2 512 "
-                     "x1 32 x1t 32 d0 32 d1 32 sw 32 n64 16 ia 32 ib 16 idf 32 idt 32 ysb 512"),
-               (U16, "rep1 8 rep8 4 offc 32 offs1 32 sc 16 offs2 32 offl 2 offv 16 offf 2 offh 2 idm 16 idl 64 r2l 2"),
-               (I32, "pI 2 ci 8")):
+for _t, _b in ((BF, "xt 520 plt 512 p2t 512 wt 512 wvt 2048 zt 656 vt 2048 at 2048 ht 2048 vals 128 nb1 16 ns1 16 e1 128 m1 128 "
+                    "s1 128 jS 1024 jV 1024 jW 1024 lst1 16 ll1 64 lwb 4 lwt 16 nb2 32 ns2 32 e32 256 m2 256 s2 256 t2 256 rr 64 "
+                    "rs 64 hd 64 keep4 128 keep8 64 win 656 tt 1088 wa 64 wb 64 wm 64 vin 256 vtr 256 r1l 2"),
+               (F32, "cf 12 ci0 48 thr 8 kc1 128 kc8 64 ic 32 iv 32 cg 16 tz1 128 tz2 256 "
+                     "xr 16 x1 32 x1t 32 d0 16 d1 16 sw 16 n64 8 ia 256 ib 32 idf 32 idt 32 ysb 512"),
+               (U16, "rep1 8 rep8 4 offp 8 offc 32 offs1 32 sc 8 offs2 32 offv 8 offx 12 offw 4 idm 16 idl 64 r0l 4 r2l 4"),
+               (I32, "pI 2 ci 12")):
     _b = _b.split()
     for _i in range(0, len(_b), 2):
         SCRATCH[_b[_i]] = ("sbuf", [128, int(_b[_i + 1])], _t)
-SEMAPHORES = ("pv psc pt pg ldx ldpl ldwv ldp2 ldw a1 l1 a2 l2 ls st sts rc1 rs1 rl1 rc2 rs2 rl2").split()
+SEMAPHORES = ("pv psc pt pg ldx ldpl ldwv ldp2 ldw a0 l0 a1 l1 a2 l2 ls st sts rc0 rs0 rl0 rc1 rs1 rl1 rc2 rs2 rl2").split()
 
-ORDER = ("pc0 pp0 pp1 mV00 pc1 mA01 mA00 eA01:v eV00:s mV20 mV30 eA00:v mV10 eV30:v eV20:s mA10 mA20 mA30 eV10:v mA11 sm eA10:s "
-         "eA20:v eA30:s mA21 mA31 qV1 qA0 eA11:s eA31:s eA21:v mO30 qV0 qA1 mO20 mO00 qA2 mO10 eO30:s mO12 mO31 mO11 eO20:s tv "
-         "eO00:s mO01 mO21 mO22 eO12:s eO01:s eO10:v eO21:s eO31:v eO22:s mO32 mO02 eO02:s qH0 eO11:v eO32:v mZ0 qH1 mZ1 eZ0 qH2 "
-         "eZ1 nb0 mZ2 eZ2 ns0 nb1 e0 ns1 m0 e1 s0 m1 t0 s1 rr0 sv t1 sg0 rr1 ov0 sg1 sw0 ov1 sc0 sw1 sca0 sc1 sca1").split()
+ORDER = ("pc0 pp0 mV00 mA00 mA01 pc1 pp1 mV30 eV00:s mV20 eV20:s eA00:v eA01:v mV10 mA10 eV30:v mA30 eV10:v eA30:v mA20 mA11 "
+         "eA10:s qV1 mA21 eA20:s mA31 qA0 eA11:s sm mO30 eA31:s qV0 eO30:s eA21:v mO20 tv mO10 mO00 qA1 mO21 eO20:s eO10:v mO01 "
+         "qA2 eO01:v mO11 mO12 eO21:v eO00:s mO31 mO02 eO12:v mO22 eO11:v eO31:s qH0 eO02:s mO32 eO22:v eO32:s mZ0 qH1 mZ1 qH2 "
+         "eZ0 mZ2 sv eZ1 eZ2").split()
 PIECES = ((0, 256), (256, 384), (384, 512))
-HALVES = ((0,), (1, 2))
 
 
 def kmap(topo, cores, s):
@@ -40,17 +39,17 @@ def kmap(topo, cores, s):
 
 def relays(topo, cores, s):
     far = kmap(topo, cores, s)[4]
-    return [c for c in topo.cores_of(cores[s]) if c != cores[s] and all(topo.may_write(c, cores[d]) for d in far)]
+    r = [c for c in topo.cores_of(cores[s]) if c != cores[s] and all(topo.may_write(c, cores[d]) for d in far)]
+    here = [c for c in r if topo.die(c) == topo.die(cores[s])]
+    return here[:1] + [c for c in r if c not in here] + here[1:]
 
 
 def bits(es):
     return sum(1 << e for e in es)
 
 
-def near_engines(topo, cores, s, d, scales=False):
-    es = topo.engines(cores[s], cores[d])
-    i = kmap(topo, cores, s)[2][d] - 4
-    return ((es[0:4], es[4:6], es[6:8]) if scales else (es[0:2], es[2:4], es[4:8]))[i]
+def shares(es, i, turned=False):
+    return ((es[0:4], es[4:6], es[6:8]) if turned else (es[0:2], es[2:4], es[4:8]))[i]
 
 
 def relay_program(g, core, T, topo):
@@ -61,21 +60,42 @@ def relay_program(g, core, T, topo):
         rl = relays(topo, C, s)
         if core not in rl[:4]:
             continue
-        d = kmap(topo, C, s)[3][rl.index(core)]
-        rid, pid = topo.addr(C[d], core)
-        es = topo.engines(core, C[d])
+        i = rl.index(core)
+        dof = kmap(topo, C, s)[3]
+        n = [0]
 
-        def go(sem, n, out, src, rsem):
-            g.wait_ge(T.sem[sem], n)
+        def go(sem, m, out, src, rsem, d):
+            rid, pid = topo.addr(C[d], core)
+            es = topo.engines(core, C[d])
+            g.wait_ge(T.sem[sem], m)
             g.remote_dma(out, src, T.sem[rsem], T.sem.ls, pid, rid, bits(es))
+            n[0] += len(es)
+
+        def two(sem, m, out, src, rsem):
+            g.wait_ge(T.sem[sem], m)
+            tr = []
+            for h in range(2):
+                d = dof[2 * (i // 2) + h]
+                rid, pid = topo.addr(C[d], core)
+                es = topo.engines(core, C[d])[4 * h:4 * h + 4]
+                tr.append(RemoteDMATransfer(dst_ids=[DstId(rid=rid, pnc=pid)], dma_engine_mask=bits(es), remote_sem=T.sem[rsem], srcs=[src(h)], dsts=[out]))
+                n[0] += len(es)
+            g.remote_dma_fused(tr, local_sem=T.sem.ls)
         a, b = 64 * s, 64 * s + 64
-        go("rc1", 4, T.clc[:, a:b].bitcast(dt.uint8), T.r1c[:, 0:64].bitcast(dt.uint8), "a1")
-        go("rs1", 4, T.cls[:, a:b], T.r1s[:, 0:64], "a1")
-        go("rl1", 2, T.ll1[:, 2 * s:2 * s + 2], T.r1l[:, 0:2], "l1")
-        go("rc2", 4, T.hlc[:, a:b].bitcast(dt.uint8), T.r2c[:, 0:64].bitcast(dt.uint8), "a2")
-        go("rs2", 4, T.hls[:, a:b], T.r2s[:, 0:64], "a2")
-        go("rl2", 2, T.idl[:, 8 * s:8 * s + 2], T.r2l[:, 0:2], "l2")
-        g.wait_ge(T.sem.ls, 6 * len(es))
+        go("rc0", 4, T.xlc[:, 32 * i:32 * i + 32].bitcast(dt.uint8), T.r0c[:, 0:32].bitcast(dt.uint8), "a0", dof[0])
+        go("rs0", 4, T.xls[:, 32 * i:32 * i + 32], T.r0s[:, 0:32], "a0", dof[0])
+        if i == 0:
+            go("rl0", 8, T.offw[:, 0:4], T.r0l[:, 0:4], "l0", dof[0])
+        else:
+            go("rc1", 4, T.clc[:, a:b].bitcast(dt.uint8), T.r1c[:, 0:64].bitcast(dt.uint8), "a1", dof[i])
+            go("rs1", 4, T.cls[:, a:b], T.r1s[:, 0:64], "a1", dof[i])
+            go("rl1", len(shares(list(range(8)), i - 1)), T.ll1[:, 8 * s:8 * s + 2], T.r1l[:, 0:2], "l1", dof[i])
+        if i in (1, 2):
+            two("rc2", 8, T.hlc[:, a:b].bitcast(dt.uint8), lambda h: T.r2c[:, 64 * h:64 * h + 64].bitcast(dt.uint8), "a2")
+        else:
+            two("rs2", 8, T.hls[:, a:b], lambda h: T.r2s[:, 64 * h:64 * h + 64], "a2")
+            two("rl2", 4, T.idl[:, 8 * s:8 * s + 2], lambda h: T.r2l[:, 2 * h:2 * h + 2], "l2")
+        g.wait_ge(T.sem.ls, n[0])
 
 
 def rank_program(g, core, T, topo):
@@ -85,7 +105,11 @@ def rank_program(g, core, T, topo):
     C = T.cores
     w3, flip, kof, dof, far = kmap(topo, C, me)
     K0 = sum(w3[b] for b in range(3) if flip >> b & 1)
-    ws = [float(-w3[b] if flip >> b & 1 else w3[b]) for b in range(3)]
+    ws = [-w3[b] if flip >> b & 1 else w3[b] for b in range(3)]
+    pi = sorted(range(3), key=lambda b: -w3[b])
+    lam, sg = ws[pi[2]], 1 if ws[pi[0]] > 0 else -1
+    d2, d3 = ws[pi[0]] // ws[pi[1]], ws[pi[1]] * lam
+    F0 = 8 * d2 * d3 * (1 - sg) + 8 * d3 + 8
     rl = relays(topo, C, me)
     Q = {"v": g.vector, "s": g.scalar, "t": g.tensor, "g": g, "y": g.sync}
     SEM = {"v": "pv", "s": "psc", "t": "pt", "g": "pg"}
@@ -116,103 +140,7 @@ def rank_program(g, core, T, topo):
         Q[q].dma_start(out, in_).then_inc(T.sem[sem], 16)
         return (sem, cnt[sem])
     v, sc, te = g.vector, g.scalar, g.tensor
-
-    ldx = load("y", "ldx", T.xt[:, 0:512], T.x[:])
-    ldpl = load("s", "ldpl", T.plt[:, 0:128], T.pl[:, 0:128])
-    W("y", ldx)
-    ldwv = load("y", "ldwv", T.wvt[:], T.wv[:])
-    ldp2 = load("y", "ldp2", T.p2t[:, 0:128], T.p2[:, 0:128])
-    ldw = load("y", "ldw", T.wt[:], T.w[:])
-
-    fl = {"allow_small_or_imprecise_dtypes": True}
-    gi = done("g", g.iota(T.pI[:, 0:1], [[0, 1]], 0, 1))
-    done("g", g.iota(T.i16[:], [[1, 16]], 0, 0, **fl))
-    gi2 = done("g", g.iota(T.kc1[:], [[0, 4], [1, 8], [0, 4]], -K0, 0, **fl))
-    done("g", g.iota(T.ic[:], [[1, 4], [64, 8]], 0, 0, **fl))
-    done("g", g.iota(T.iv[:], [[32, 16], [0, 2]], -256, 0, **fl))
-    done("g", g.iota(T.iw[:], [[128, 8], [0, 4]], 0, 0, **fl))
-    gi3 = done("g", g.iota(T.kc8[:], [[0, 8], [1, 8]], -K0, 0, **fl))
-    zx = V(v.memset(T.xt[:, 512:520], 0.0))
-    V(v.memset(T.nb1[:, 0:16:4], 0.0))
-    for b in range(4):
-        V(v.memset(T.keep4[:, b:32:4], float(min(b, 1))))
-        rep1 = V(v.memset(T.rep1[:, 2 * b:2 * b + 2], 4 * b + 3))
-    W("v", gi)
-    V(v.tensor_scalar(T.ci[:, 0:1], T.pI[:, 0:1], 31, None, OP.bitwise_and))
-    V(v.tensor_scalar(T.ci[:, 1:2], T.pI[:, 0:1], 3, None, OP.bitwise_and))
-    V(v.tensor_scalar(T.ci[:, 2:3], T.pI[:, 0:1], 15, None, OP.bitwise_and))
-    c0 = V(v.tensor_scalar(T.ci[:, 3:4], T.pI[:, 0:1], 4, 1, OP.arith_shift_right, OP.bitwise_and))
-    W("v", c0)
-    c0 = V(v.tensor_copy(T.cf[:, 0:4], T.ci[:, 0:4]))
-    W("v", c0)
-    lane, u4, l16, mO, par, b3, l2 = (T.cf[:, i:i + 1] for i in range(7))
-    c2 = V(v.tensor_scalar(T.u16[:, 0:1], u4, 16.0, 0.5, OP.mult, OP.add))
-    c3 = V(v.tensor_scalar(T.offl[:, 0:1], l16, 2.0, mO, OP.mult, OP.add))
-    nS = 6
-    W("v", c2, gi2)
-    thr = V(v.tensor_scalar(T.thr[:], T.i16[:], T.u16[:, 0:1], None, OP.add))
-
-    W("v", ldpl)
-    for a in range(1, 4):
-        k = V(v.tensor_copy(T.plt[:, 128 * a:128 * a + 128], T.plt[:, 0:128]))
-    W("v", k)
-    qpl = V(v.quantize_mx(T.plqc[:, 0:128], T.plqs[:, 0:128], T.plt[:, 0:512]))
-    W("v", ldx, zx)
-    qx = V(v.quantize_mx(T.xqc[:, 0:130], T.xqs[:, 0:130], T.xt[:, 0:520]))
-
-    def mm(out, n, l, lo, r, ro):
-        return done("t", te.matmul_mx(T.ps[:, out:out + n], T[l + "c"][:, lo:lo + 128], T[l + "s"][:, lo:lo + 128],
-                                      T[r + "c"][:, ro:ro + n], T[r + "s"][:, ro:ro + n], True, True))
-    W("t", qpl, qx)
-    z = mm(0, 128, "plq", 0, "xq", 0)
-    W("v", z, rep1)
-    z1 = V(v.transpose(T.tz1[:], T.ps[:, 0:128]))
-    W("v", z1)
-    for b in range(3):
-        k = V(v.tensor_scalar(T.nb1[:, b + 1:16:4], T.tz1[:, b:128:32], 0.0, ws[b], OP.is_lt, OP.mult))
-    W("v", k)
-    k = V(v.tensor_tensor_scan(T.ns1[:], T.keep4[:, 0:16], T.nb1[:], 0.0, OP.mult, OP.add))
-    W("v", k, gi2)
-    k = V(v.tensor_tensor(T.e1[:], T.ns1[:, 0:16].indirect(T.rep1[:, 0:8]), T.kc1[:], OP.is_equal))
-    W("v", k)
-    k = V(v.transpose(T.m1[:], T.e1[:]))
-    W("v", k)
-    k = V(v.tensor_tensor_scan(T.s1[:], T.m1[:], T.m1[:], 0.0, OP.add, OP.max))
-    W("s", k, thr)
-    W("v", k, thr)
-    for i in range(nS):
-        ks = S(sc.activation(T.jS[:, 128 * i:128 * i + 128], T.s1[:], AF.Sign, bias=T.thr[:, i:i + 1], scale=-1.0, accum_out=T.x1[:, i:i + 1]))
-    nV = 128 * (16 - nS)
-    for i in range(nS, 16):
-        k = V(v.tensor_scalar(T.jV[:, 128 * (i - nS):128 * (i - nS) + 128], T.s1[:], T.thr[:, i:i + 1], None, OP.is_gt))
-    W("v", k)
-    k = V(v.tensor_tensor_scan(T.jW[:, 0:nV], T.jV[:, 0:nV], T.jV[:, 0:nV], 0.0, OP.mult, OP.add))
-    W("v", k)
-    for a in (0, 16):
-        V(v.tensor_scalar(T.x1[:, a + nS:a + 16], T.jW[:, 127:nV:128], -2.0, 128.0, OP.mult, OP.add))
-    W("v", ks)
-    k = V(v.tensor_copy(T.x1[:, 16:16 + nS], T.x1[:, 0:nS]))
-    W("v", k)
-    k = V(v.transpose(T.x1t[:], T.x1[:]))
-    W("v", k, c3)
-    of1 = V(v.tensor_scalar(T.offs1[:], T.x1t[:], 0.5, 64.0, OP.mult, OP.add))
-    W("v", of1)
-    W("s", of1)
-
-    def pickc(out, a, b, src, n, off, e, f):
-        return V(v.tensor_copy(T[out + "c"][:, a:b].bitcast(dt.uint32), T[src + "c"][:, 0:n].bitcast(dt.uint32).indirect(T[off][:, e:f])))
-
-    def picks(out, a, b, src, n, off, e, f):
-        return S(sc.activation(T[out + "s"][:, a:b], T[src + "s"][:, 0:n].indirect(T[off][:, e:f]), AF.Copy))
-    own = 64 * me
-    c1r = pickc("sl1r", 0, 256, "xq", 130, "offs1", 0, 16)
-    s1r = picks("sl1r", 0, 256, "xq", 130, "offs1", 0, 16)
-    c1d = pickc("sl1d", 0, 192, "xq", 130, "offs1", 16, 28)
-    s1d = picks("sl1d", 0, 192, "xq", 130, "offs1", 16, 28)
-    c1o = pickc("cl", own, own + 64, "xq", 130, "offs1", 28, 32)
-    s1o = picks("cl", own, own + 64, "xq", 130, "offs1", 28, 32)
-    l1 = V(v.tensor_scalar(T.lst1[:], T.x1t[:, 0:32].indirect(T.offl[:, 0:1]), 0.5, 64.0, OP.mult, OP.add))
-
+    ts, tt = v.tensor_scalar, v.tensor_tensor
     lsn = [0]
 
     def fused(parts):
@@ -223,80 +151,214 @@ def rank_program(g, core, T, topo):
             lsn[0] += len(es)
         g.remote_dma_fused(tr, local_sem=T.sem.ls)
 
-    def far_parts(src, dst, sem, lst=False):
-        es = [topo.engines(core, c) for c in rl[:4]]
-        return [(rl[i], es[i][8 + 2 * i:10 + 2 * i] if lst else es[i][4 * i:4 * i + 4], src(i), dst, sem) for i in range(4)]
-
-    def near_parts(src, dst, sem, scales=False):
-        return [(C[dof[4 + i]], near_engines(topo, C, me, dof[4 + i], scales), src(i), dst, sem) for i in range(3)]
-
     def u8(t, a, b):
         return T[t][:, a:b].bitcast(dt.uint8)
-    W("g", c1r)
-    fused(far_parts(lambda i: u8("sl1rc", 64 * i, 64 * i + 64), u8("r1c", 0, 64), "rc1"))
-    W("g", s1r)
-    fused(far_parts(lambda i: T.sl1rs[:, 64 * i:64 * i + 64], T.r1s[:, 0:64], "rs1"))
-    W("g", c1d)
-    fused(near_parts(lambda i: u8("sl1dc", 64 * i, 64 * i + 64), u8("clc", own, own + 64), "a1"))
-    W("g", s1d)
-    fused(near_parts(lambda i: T.sl1ds[:, 64 * i:64 * i + 64], T.cls[:, own:own + 64], "a1", True))
-    W("g", l1)
-    fused(far_parts(lambda i: T.lst1[:, 2 * i:2 * i + 2], T.r1l[:, 0:2], "rl1", True))
-    fused(near_parts(lambda i: T.lst1[:, 8 + 2 * i:10 + 2 * i], T.ll1[:, 2 * me:2 * me + 2], "l1"))
 
-    W("v", gi3, c0)
-    V(v.tensor_scalar(T.ci[:, 4:5], T.pI[:, 0:1], 1, None, OP.bitwise_and))
-    V(v.tensor_scalar(T.ci[:, 5:6], T.pI[:, 0:1], 3, 1, OP.arith_shift_right, OP.bitwise_and))
-    V(v.tensor_scalar(T.ci[:, 6:7], T.pI[:, 0:1], 1, 7, OP.arith_shift_right, OP.bitwise_and))
-    V(v.memset(T.vin[:], 0.0))
-    k = V(v.memset(T.zt[:], 0.0))
+    def pickc(out, a, b, src, n, off, e, f):
+        return V(v.tensor_copy(T[out + "c"][:, a:b].bitcast(dt.uint32), T[src + "c"][:, 0:n].bitcast(dt.uint32).indirect(T[off][:, e:f])))
+
+    def picks(out, a, b, src, n, off, e, f):
+        return S(sc.activation(T[out + "s"][:, a:b], T[src + "s"][:, 0:n].indirect(T[off][:, e:f]), AF.Copy))
+
+    def quant(n, t, a, b, *deps):
+        W("v", *deps)
+        return V(v.quantize_mx(T[n + "c"][:, a:b], T[n + "s"][:, a:b], T[t][:, 4 * a:4 * b]))
+
+    def mm(out, n, l, lo, r, ro):
+        return done("t", te.matmul_mx(T.ps[:, out:out + n], T[l + "c"][:, lo:lo + 128], T[l + "s"][:, lo:lo + 128],
+                                      T[r + "c"][:, ro:ro + n], T[r + "s"][:, ro:ro + n], True, True))
+    out_ = topo.engines(core, C[dof[4]])
+    in_ = [e for e in topo.engines(core, rl[0]) if e not in out_]
+    all_ = out_ + in_
+
+    ldx = load("y", "ldx", T.xt[:, 0:512], T.x[:])
+    ldpl = load("s", "ldpl", T.plt[:, 0:16], T.pl[:, 0:16])
+    ldwv = load("y", "ldwv", T.wvt[:], T.wv[:])
+    ldp2 = load("y", "ldp2", T.p2t[:, 0:16], T.p2[:, 0:16])
+
+    fl = {"allow_small_or_imprecise_dtypes": True}
+    three, i16 = T.ci0[:, 0:4], T.ci0[:, 32:48]
+    gi = done("g", g.iota(T.pI[:, 0:1], [[0, 1]], 0, 1))
+    gi1 = done("g", g.iota(three, [[0, 4]], 3, 0, **fl))
+    done("g", g.iota(T.ci0[:, 8:16], [[4, 8]], 1, 0, **fl))
+    done("g", g.iota(T.ci0[:, 16:24], [[4, 4], [0, 2]], 3, 0, **fl))
+    gi2 = done("g", g.iota(T.kc1[:], [[0, 4], [lam, 8], [0, 4]], F0 - lam * K0, 0, **fl))
+    done("g", g.iota(i16, [[1, 16]], 0, 0, **fl))
+    done("g", g.iota(T.ic[:], [[1, 4], [64, 8]], 0, 0, **fl))
+    done("g", g.iota(T.iv[:, 0:16], [[32, 8], [0, 2]], -256, 0, **fl))
+    done("g", g.iota(T.iv[:, 16:32], [[128, 4], [0, 4]], 0, 0, **fl))
+    gi3 = done("g", g.iota(T.kc8[:], [[0, 8], [lam, 8]], F0 - lam * K0, 0, **fl))
+    zp = V(v.memset(T.plt[:, 16:512], 0.0))
+    W("v", gi)
+
+    def field(i, shift, mask):
+        if shift:
+            return V(ts(T.ci[:, i:i + 1], T.pI[:, 0:1], shift, mask, OP.arith_shift_right, OP.bitwise_and))
+        return V(ts(T.ci[:, i:i + 1], T.pI[:, 0:1], mask, None, OP.bitwise_and))
+    field(0, 0, 15), field(1, 0, 3), field(2, 5, 2)
+    c0 = field(3, 4, 1)
+    zx = V(v.memset(T.xt[:, 512:520], 0.0))
+    W("v", c0)
+    c0 = V(v.tensor_copy(T.cf[:, 0:4], T.ci[:, 0:4]))
+    for b, x in enumerate((0, -sg, d2, d3)):
+        V(v.memset(T.hd[:, b:64:4], float(x)))
+    W("v", c0)
+    l16, u4, h2, mO, lane, par, b3, l2, l4, l2m, h32 = (T.cf[:, i:i + 1] for i in range(11))
+    cg = [T.cg[:, i:i + 1] for i in range(16)]
+    V(ts(cg[0], l16, 8.0, float(pi[0] - 3), OP.is_equal, OP.mult))
+    V(ts(cg[1], l16, 0.0, float(pi[1] - 3), OP.is_equal, OP.mult))
+    c1 = V(ts(cg[2], l16, 8.0, float(pi[2] - 3), OP.is_equal, OP.mult))
+    c2 = V(ts(cg[3], u4, 32.0, h2, OP.mult, OP.add))
+    W("v", c1, gi1)
+    V(ts(T.offp[:, 0:8:2], three, cg[0], None, OP.add))
+    c1 = V(ts(T.offp[:, 1:8:2], three, cg[1], cg[2], OP.add, OP.add))
+    W("v", c2, gi2)
+    V(ts(T.thr[:], T.ci0[:, 8:16], cg[3], None, OP.add))
+    V(ts(T.offx[:, 0:1], l16, 2.0, mO, OP.mult, OP.add))
+    c3 = V(v.tensor_copy(T.rep1[:], T.ci0[:, 16:24]))
+
+    qpl = quant("plq", "plt", 0, 128, ldpl, zp)
+    W("v", qpl, c1)
+    W("s", qpl, c1)
+    ppc, pps = pickc("plp", 0, 128, "plq", 128, "offp", 0, 8), picks("plp", 0, 128, "plq", 128, "offp", 0, 8)
+    qx = quant("xq", "xt", 0, 130, ldx, zx)
+    W("g", qx)
+    fused([(rl[i], all_[4 * i:4 * i + 4], u8("xqc", 32 * i, 32 * i + 32), u8("r0c", 0, 32), "rc0") for i in range(4)])
+    fused([(rl[i], all_[4 * i:4 * i + 4], T.xqs[:, 32 * i:32 * i + 32], T.r0s[:, 0:32], "rs0") for i in range(4)])
+    W("t", ppc, pps, qx)
+    z = mm(0, 128, "plp", 0, "xq", 0)
+    W("v", z, c3)
+    z1 = V(v.transpose(T.tz1[:], T.ps[:, 0:128]))
+    W("v", z1)
+    k = V(ts(T.nb1[:], T.tz1[:, 0:128:8], 0.0, 8.0, OP.is_lt, OP.add))
     W("v", k)
-    V(v.tensor_copy(T.cf[:, 4:7], T.ci[:, 4:7]))
-    V(v.tensor_scalar(T.cg[:, 0:1], l16, 4.0, None, OP.mult))
-    V(v.tensor_scalar(T.cg[:, 1:2], l16, 0.0, 256.0, OP.is_equal, OP.mult))
-    V(v.tensor_scalar(T.cg[:, 2:3], mO, -33.0, 17.0, OP.mult, OP.add))
-    k = V(v.tensor_scalar(T.cg[:, 3:4], mO, 16.0, None, OP.mult))
+    k = V(v.tensor_tensor_scan(T.ns1[:], T.hd[:, 0:16], T.nb1[:], 0.0, OP.mult, OP.add))
+    W("v", k)
+    k = V(tt(T.e1[:], T.ns1[:, 0:16].indirect(T.rep1[:, 0:8]), T.kc1[:], OP.is_equal))
+    W("v", k)
+    k = V(v.transpose(T.m1[:], T.e1[:]))
+    W("v", k)
+    k = V(v.tensor_tensor_scan(T.s1[:], T.m1[:], T.m1[:], 0.0, OP.add, OP.max))
+    W("s", k)
+    W("v", k)
+    nS = 3
+    for i in range(nS):
+        ks = S(sc.activation(T.jS[:, 128 * i:128 * i + 128], T.s1[:], AF.Sign, bias=T.thr[:, i:i + 1], scale=-2.0, accum_out=T.xr[:, i:i + 1]))
+    nV = 128 * (8 - nS)
+    for i in range(nS, 8):
+        k = V(ts(T.jV[:, 128 * (i - nS):128 * (i - nS) + 128], T.s1[:], 2.0, T.thr[:, i:i + 1], OP.mult, OP.is_gt))
+    W("v", k)
+    k = V(v.tensor_tensor_scan(T.jW[:, 0:nV], T.jV[:, 0:nV], T.jV[:, 0:nV], 0.0, OP.mult, OP.add))
+    W("v", k)
+    for a in (0, 8):
+        V(ts(T.xr[:, a + nS:a + 8], T.jW[:, 127:nV:128], -2.0, 128.0, OP.mult, OP.add))
+    W("v", ks)
+    k = V(v.tensor_copy(T.xr[:, 8:8 + nS], T.xr[:, 0:nS]))
+    W("v", k)
+    for a in (0, 64):
+        for b in range(2):
+            k = V(v.tensor_copy(T.x1[a:a + 64, b:32:2], T.xr[64 * b:64 * b + 64, 0:16]))
+    W("v", k)
+    k = V(v.transpose(T.x1t[:], T.x1[:]))
+    W("v", k)
+    of1 = V(ts(T.offs1[:], T.x1t[:], 0.5, 64.0, OP.mult, OP.add))
+    W("v", of1)
+    W("s", of1)
+    own = 64 * me
+    c1r = pickc("sl1r", 0, 256, "xq", 130, "offs1", 4, 20)
+    s1r = picks("sl1r", 0, 256, "xq", 130, "offs1", 4, 20)
+    c1d = pickc("sl1d", 0, 128, "xq", 130, "offs1", 20, 28)
+    s1d = picks("sl1d", 0, 128, "xq", 130, "offs1", 20, 28)
+    l1 = V(ts(T.lst1[:], T.x1t[:, 0:32].indirect(T.offx[:, 0:1]), 0.5, 64.0, OP.mult, OP.add))
+    c1o = pickc("cl", own, own + 64, "xq", 130, "offs1", 28, 32)
+    s1o = picks("cl", own, own + 64, "xq", 130, "offs1", 28, 32)
+
+    W("g", of1)
+    fused([(rl[0], in_, T.offs1[:, 0:4], T.r0l[:, 0:4], "rl0")])
+    W("g", c1r)
+    fused([(rl[i], all_[4 * i:4 * i + 4], u8("sl1rc", 64 * i - 64, 64 * i), u8("r1c", 0, 64), "rc1") for i in range(1, 4)]
+          + [(C[dof[4]], out_[0:4], u8("sl1rc", 192, 256), u8("clc", own, own + 64), "a1")])
+    W("g", s1r)
+    fused([(rl[i], all_[4 * i:4 * i + 4], T.sl1rs[:, 64 * i - 64:64 * i], T.r1s[:, 0:64], "rs1") for i in range(1, 4)]
+          + [(C[dof[4]], out_[0:4], T.sl1rs[:, 192:256], T.cls[:, own:own + 64], "a1")])
+    W("g", c1d)
+    fused([(C[dof[5 + i]], out_[4 * i:4 * i + 4], u8("sl1dc", 64 * i, 64 * i + 64), u8("clc", own, own + 64), "a1") for i in range(2)])
+    W("g", s1d)
+    fused([(C[dof[5 + i]], out_[4 * i:4 * i + 4], T.sl1ds[:, 64 * i:64 * i + 64], T.cls[:, own:own + 64], "a1") for i in range(2)])
+    W("g", l1)
+    fused([(rl[i], shares(in_, i - 1), T.lst1[:, 2 * i:2 * i + 2], T.r1l[:, 0:2], "rl1") for i in range(1, 4)])
+    fused([(C[dof[4 + i]], shares(out_, i), T.lst1[:, 8 + 2 * i:10 + 2 * i], T.ll1[:, 8 * me:8 * me + 2], "l1") for i in range(3)])
+
+    W("v", gi3, l1)
+    V(v.memset(T.zt[:], 0.0))
+    field(4, 0, 31), field(5, 0, 1), field(6, 3, 1), field(7, 1, 7), field(8, 2, 3), field(9, 1, 3), field(10, 1, 32)
+    V(v.tensor_copy(T.ll1[:, 8 * me:8 * me + 2], T.lst1[:, 14:16]))
+    V(ts(T.offx[:, 2:3], T.offx[:, 0:1], 3.0, None, OP.min))
+    V(ts(T.keep4[:], T.kc1[:], -1000.0, None, OP.is_ge))
+    V(ts(cg[4], l16, 4.0, None, OP.mult))
+    V(ts(cg[5], l16, 0.0, 256.0, OP.is_equal, OP.mult))
+    V(ts(cg[6], mO, -17.0, 9.0, OP.mult, OP.add))
+    k = V(ts(cg[7], mO, 8.0, None, OP.mult))
     W("v", k)
     W("s", k)
-    wi = S(sc.activation(T.win[:], T.zt[:, 0:784], AF.Identity, bias=T.cg[:, 1:2]))
-    oc_ = V(v.tensor_scalar(T.offc[:], T.ic[:], T.cg[:, 0:1], None, OP.add))
-    V(v.tensor_scalar(T.cg[:, 4:5], b3, 4.0, 3.0, OP.mult, OP.add))
-    V(v.tensor_scalar(T.cg[:, 5:6], par, T.cg[:, 2:3], T.cg[:, 3:4], OP.mult, OP.add))
-    W("v", ldwv)
-    qwv = V(v.quantize_mx(T.wvqc[:, 0:512], T.wvqs[:, 0:512], T.wvt[:, 0:2048]))
-    W("v", qwv)
-    V(v.tensor_scalar(T.rep8[:], T.i16[:, 0:4], 8.0, T.cg[:, 4:5], OP.mult, OP.add))
-    V(v.tensor_scalar(T.offh[:], T.i16[:, 0:2], 8.0, l2, OP.mult, OP.add))
-    V(v.tensor_scalar(T.offv[:], T.i16[:], 32.0, lane, OP.mult, OP.add))
-    V(v.tensor_scalar(T.vin[:, 0:512:16], T.iv[:], lane, None, OP.add))
-    V(v.tensor_copy(T.vin[:, 2:512:16], T.iw[:]))
-    V(v.tensor_scalar(T.keep8[:], T.kc8[:], 0.5 - K0, None, OP.is_gt))
-    V(v.memset(T.d0[:, 0:32:2], 1000000.0))
-    V(v.memset(T.e32[:], 0.0))
-    V(v.memset(T.idf[:, 16:32], 0.0))
-    V(v.tensor_scalar(T.idu[:], T.i16[:], 16.0, 512.0, OP.mult, OP.add))
-    k = V(v.tensor_tensor(T.cg[:, 6:7], T.cg[:, 5:6], l2, OP.add))
-    W("v", k, ldp2)
-    V(v.tensor_scalar(T.offf[:], T.i16[:, 0:2], 8.0, T.cg[:, 6:7], OP.mult, OP.add))
-    V(v.tensor_scalar(T.d1[:, 1:32:2], T.idu[:], l16, None, OP.add))
-    for a in range(1, 4):
-        k = V(v.tensor_copy(T.p2t[:, 128 * a:128 * a + 128], T.p2t[:, 0:128]))
-    W("v", k, ldw)
+    zv = S(sc.activation(T.vin[:], T.zt[:, 0:256], AF.Copy))
+    zp2 = S(sc.activation(T.p2t[:, 16:512], T.zt[:, 0:496], AF.Copy))
+    S(sc.activation(T.e32[:], T.zt[:, 0:256], AF.Copy))
+    wi = S(sc.activation(T.win[:], T.zt[:], AF.Identity, bias=cg[5]))
+    k = V(v.tensor_copy(T.cf[:, 4:11], T.ci[:, 4:11]))
+    V(v.quantize_mx(T.xlc[:, 128:256], T.xls[:, 128:256], T.zt[:, 0:512]))
     V(v.quantize_mx(T.hqc[:, 512:640], T.hqs[:, 512:640], T.zt[:, 0:512]))
-    qp2 = V(v.quantize_mx(T.p2qc[:, 0:128], T.p2qs[:, 0:128], T.p2t[:, 0:512]))
-    qw = V(v.quantize_mx(T.wqc[:, 0:128], T.wqs[:, 0:128], T.wt[:, 0:512]))
+    W("v", k)
+    V(ts(T.offc[:], T.ic[:], cg[4], None, OP.add))
+    V(ts(cg[8], b3, 4.0, 3.0, OP.mult, OP.add))
+    V(ts(cg[9], par, cg[6], cg[7], OP.mult, OP.add))
+    V(ts(cg[10], l4, 6.0, l2, OP.mult, OP.add))
+    V(ts(cg[11], l2m, 8.0, par, OP.mult, OP.add))
+    V(ts(cg[12], h32, 8.0, lane, OP.mult, OP.add))
+    V(ts(cg[13], h32, 16.0, None, OP.mult))
+    V(ts(cg[14], l16, 512.0, None, OP.add))
+    V(ts(T.offv[:], T.ci0[:, 32:40], 32.0, lane, OP.mult, OP.add))
+    V(ts(T.keep8[:], T.kc8[:], float(F0 - lam * K0), None, OP.not_equal))
+    V(v.memset(T.keep4[:, 0:128:4], 0.0))
+    V(v.memset(T.d0[:, 0:16:2], 1000000.0))
+    V(v.memset(T.idf[0:32, 16:32], 0.0))
+    k = V(v.memset(T.idm[64:128, 0:16], 0))
+    W("v", k, zv)
+    V(ts(T.rep8[:], T.ci0[:, 32:36], 8.0, cg[8], OP.mult, OP.add))
+    V(ts(T.offx[:, 4:5], cg[9], l2, None, OP.add))
+    V(ts(T.offx[:, 6:7], cg[10], h32, None, OP.add))
+    V(ts(T.offx[:, 8:9], cg[11], h32, None, OP.add))
+    V(ts(T.vin[:, 0:256:16], T.iv[:, 0:16], cg[12], None, OP.add))
+    V(ts(T.vin[:, 9:256:16], T.iv[:, 16:32], cg[13], None, OP.add))
+    V(ts(T.d1[:, 1:16:2], T.ci0[:, 32:40], 16.0, cg[14], OP.mult, OP.add))
+    k = quant("p2q", "p2t", 0, 128, ldp2, zp2)
+    qwv = quant("wvq", "wvt", 0, 512, ldwv)
+    W("v", k)
+    W("s", k)
+    p2c, p2s = pickc("p2p", 0, 128, "p2q", 128, "offp", 0, 8), picks("p2p", 0, 128, "p2q", 128, "offp", 0, 8)
 
-    nd, ndl, nf = 0, 0, 0
-    for s in range(8):
-        if s in far:
-            nf += len(topo.engines(relays(topo, C, s)[kmap(topo, C, s)[2][me]], core))
-        elif s != me:
-            ndl += len(near_engines(topo, C, s, me))
-            nd += len(near_engines(topo, C, s, me)) + len(near_engines(topo, C, s, me, True))
-    a1 = ("a1", nd + 2 * nf)
-    W("v", a1, c1o, s1o, qw)
-    W("s", a1, c1o, s1o, qw)
-    W("t", a1, c1o, s1o, qw)
+    ks_ = [kmap(topo, C, s)[2][me] for s in range(8)]
+    s0 = ks_.index(0)
+    ne = [len(topo.engines(relays(topo, C, s)[ks_[s]], core)) if s in far else 0 for s in range(8)]
+    W("v", ("a0", 8 * ne[s0]), ("l0", ne[s0]), p2c)
+    W("s", ("a0", 8 * ne[s0]), ("l0", ne[s0]), p2c)
+    c0o = pickc("cl", 64 * s0, 64 * s0 + 64, "xl", 130, "offw", 0, 4)
+    s0o = picks("cl", 64 * s0, 64 * s0 + 64, "xl", 130, "offw", 0, 4)
+    k = V(v.tensor_copy(T.lwb[:], T.offw[:]))
+    W("v", k)
+    k = V(v.tensor_copy(T.lwt[:], T.lwb[:, 0:4].indirect(T.offx[:, 2:3])))
+    W("v", k)
+    l0 = V(v.tensor_copy(T.ll1[:, 8 * s0:8 * s0 + 2], T.lwt[:, 0:2]))
+
+    nf = sum(ne)
+    nl = sum(len(shares(out_, ks_[s] - 4)) for s in range(8) if 4 <= ks_[s] < 7)
+    nd = nl + sum(len(shares(out_, ks_[s] - 4, True)) for s in range(8) if 4 <= ks_[s] < 7)
+    a1 = ("a1", 24 + 2 * (nf - ne[s0]))
+    W("v", a1, c1o, s1o, c0o, s0o)
+    W("s", a1, c1o, s1o, c0o, s0o)
+    W("t", a1, c1o, s1o, c0o, s0o)
+    W("y", a1)
+    ldw = load("y", "ldw", T.wt[:], T.w[:])
     D, bank, users = {}, {}, [z1] + [None] * 7
 
     def product(x, n, l, lo, r, ro, *deps):
@@ -311,15 +373,11 @@ def rank_program(g, core, T, topo):
         if q == "s":
             k = S(sc.activation(out, src, func, scale=scale))
         elif func == AF.Relu:
-            k = V(v.tensor_scalar(out, src, 0.0, scale, OP.max, OP.mult))
+            k = V(ts(out, src, 0.0, scale, OP.max, OP.mult))
         else:
-            k = V(v.tensor_copy(out, src) if scale == 1.0 else v.tensor_scalar(out, src, scale, None, OP.mult))
+            k = V(v.tensor_copy(out, src) if scale == 1.0 else ts(out, src, scale, None, OP.mult))
         users[bank[x]] = k
         return k
-
-    def quant(n, t, a, b, *deps):
-        W("v", *deps)
-        return V(v.quantize_mx(T[n + "c"][:, a:b], T[n + "s"][:, a:b], T[t][:, 4 * a:4 * b]))
 
     for x in ORDER:
         x, q = (x + ":").split(":")[:2]
@@ -347,112 +405,115 @@ def rank_program(g, core, T, topo):
         elif x[:2] == "qH":
             D[x] = quant("hq", "ht", a, b, *[D["eO%d%d" % (i, j)] for i in range(4)])
         elif x[:2] == "mZ":
-            D[x] = product(x[1:], b - a, "p2q", 0, "hq", a, D["qH%d" % j])
+            D[x] = product(x[1:], b - a, "p2p", 0, "hq", a, D["qH%d" % j])
         elif x[:2] == "eZ":
             W("v", D["m" + x[1:]])
-            D[x] = users[bank[x[1:]]] = V(v.transpose(T.tz2[:, a:b], T.ps[:, 512 * bank[x[1:]]:512 * bank[x[1:]] + b - a]))
+            r, o = 64 * (a // 256), 512 * bank[x[1:]]
+            D[x] = users[bank[x[1:]]] = V(v.transpose(T.tz2[r:r + 64, a % 256:a % 256 + b - a], T.ps[r:r + 64, o:o + b - a]))
         elif x == "sm":
-            W("s", ("l1", ndl + nf), l1)
-            k = S(sc.activation(T.ll1[:, 2 * me:2 * me + 2], T.lst1[:, 14:16], AF.Copy))
-            W("s", k)
-            S(sc.activation(T.vin[:, 1:512:16], T.ll1[:, 0:16].indirect(T.offh[:, 0:2]), AF.Identity, bias=1.0))
-            D[x] = S(sc.activation(T.nb2[:, 0:64:4], T.ll1[:], AF.Relu, bias=-12700.0, scale=100.0))
+            W("s", ("l1", nl + nf - ne[s0]), l0)
+            S(sc.activation(T.vin[:, 1:256:16], T.ll1[:, 0:64].indirect(T.offx[:, 6:7]), AF.Identity, bias=1.0))
+            D[x] = S(sc.activation(T.hd[:, 1:64:4], T.ll1[:, 0:64].indirect(T.offx[:, 8:9]), AF.Sign, bias=-127.5 * sg, scale=float(sg)))
         elif x == "tv":
             W("v", D["sm"])
             D[x] = V(v.transpose(T.vtr[:], T.vin[:]))
-        elif x == "sv":
-            W("s", D["tv"])
-            D[x] = S(sc.activation(T.vals[:], T.vtr[:, 0:512].indirect(T.offv[:, 0:16]), AF.Copy))
-        elif x[:2] == "nb":
-            W("v", D["sm"], *[D["eZ%d" % h] for h in HALVES[j]])
-            for i in range(3):
-                D[x] = V(v.tensor_scalar(T.nb2[:, 32 * j + 1 + i:32 * j + 32:4], T.tz2[:, p0 + i:p1:32], 0.0, ws[i], OP.is_lt, OP.mult))
-        elif x[:2] == "ns":
-            W("v", D["nb%d" % j])
-            D[x] = V(v.tensor_tensor_scan(T.ns2[:, 32 * j:32 * j + 32], T.keep4[:], T.nb2[:, 32 * j:32 * j + 32], 0.0, OP.mult, OP.add))
-        elif x[:2] == "rr":
-            W("v", D["t%d" % j])
-            V(v.tensor_scalar(T.n64[:, 8 * j:8 * j + 8], T.ns2[:, 32 * j + 3:32 * j + 32:4], 64.0, 64.0 * K0 - 1.0, OP.mult, OP.add))
-            D[x] = V(v.tensor_tensor(T.rr[:, 64 * j:64 * j + 64], T.t2[:, p0:p1:4], T.e32[:, p0:p1:4], OP.mult))
-        elif x[:2] == "sg":
-            W("v", D["rr%d" % j])
-            D[x] = V(v.tensor_tensor_scan(T.rs[:, 64 * j:64 * j + 64], T.keep8[:], T.rr[:, 64 * j:64 * j + 64], 0.0, OP.mult, OP.add))
-        elif x[:2] == "ov":
-            W("v", D["sg%d" % j])
-            r = T.rs[:, 64 * j + 7:64 * j + 64:8]
-            V(v.tensor_scalar(T.d0[:, 16 * j + 1:16 * j + 16:2], r, 64.5, 5000.0, OP.is_gt, OP.mult))
-            D[x] = V(v.tensor_tensor(T.d1[:, 16 * j:16 * j + 16:2], r, T.n64[:, 8 * j:8 * j + 8], OP.add))
-        elif x[:2] == "sw":
-            W("v", D["ov%d" % j])
-            D[x] = V(v.tensor_tensor_scan(T.sw[:, 16 * j:16 * j + 16], T.d0[:, 16 * j:16 * j + 16], T.d1[:, 16 * j:16 * j + 16], 0.0, OP.add, OP.min))
-        elif x[:3] == "sca":
-            W("v", D["sc%d" % j], D["sv"], wi, *([D["sca0"]] if j else []))
-            D[x] = V(v.tensor_copy(T.win[:, 16:784].indirect(T.sc[:, 8 * j:8 * j + 8]), T.vals[:, 128 * j:128 * j + 128]))
-        elif x[:2] == "sc":
-            W("v", D["sw%d" % j])
-            D[x] = V(v.tensor_copy(T.sc[:, 8 * j:8 * j + 8], T.sw[:, 16 * j + 1:16 * j + 16:2]))
-        elif x[0] == "e":
-            W("v", D["ns%d" % j])
-            D[x] = V(v.tensor_tensor(T.e32[:, p0:p1:4], T.ns2[:, 32 * j:32 * j + 32].indirect(T.rep8[:, 0:4]), T.kc8[:], OP.is_equal))
-        elif x[0] == "m":
-            W("v", D["e%d" % j])
-            D[x] = V(v.transpose(T.m2[:, p0:p1], T.e32[:, p0:p1]))
-        elif x[0] == "s":
-            W("v", D["m%d" % j], *([D["s0"]] if j else []))
-            D[x] = V(v.tensor_tensor_scan(T.s2[:, p0:p1], T.m2[:, p0:p1], T.m2[:, p0:p1], T.s2[:, 255:256] if j else 0.0, OP.add, OP.max))
         else:
-            W("v", D["s%d" % j])
-            D[x] = V(v.transpose(T.t2[:, p0:p1], T.s2[:, p0:p1]))
-    W("v", D["sca1"])
-    V(v.transpose(T.tt[:, 0:512], T.win[:, 16:528]))
-    k = V(v.transpose(T.tt[:, 512:1056], T.win[:, 0:544]))
+            W("s", D["tv"])
+            D[x] = S(sc.activation(T.vals[:], T.vtr[:, 0:256].indirect(T.offv[:, 0:8]), AF.Copy))
+    W("v", D["eZ2"])
+    k = V(ts(T.nb2[:], T.tz2[:, 0:256:8], 0.0, 8.0, OP.is_lt, OP.add))
     W("v", k)
-    k = V(v.tensor_tensor(T.wm[:, 0:33], T.tt[:, 0:1056:32], T.tt[:, 16:1056:32], OP.min))
+    k = V(v.tensor_tensor_scan(T.ns2[:], T.hd[:, 0:32], T.nb2[:], 0.0, OP.mult, OP.add))
     W("v", k)
-    of2 = V(v.tensor_scalar(T.offs2[:], T.wm[:, 0:33].indirect(T.offf[:, 0:2]), 256.0, None, OP.add))
-    W("v", of2)
-    W("s", of2)
+    W("s", k)
+    n64 = S(sc.activation(T.n64[:], T.ns2[:, 3:32:4], AF.Identity, bias=64.0 * (K0 - lam * F0) - 1.0, scale=64.0 * lam))
+    k = V(tt(T.e32[:, 0:256:4], T.ns2[:, 0:32].indirect(T.rep8[:, 0:4]), T.kc8[:], OP.is_equal))
+    W("v", k)
+    k = V(v.transpose(T.m2[:], T.e32[:]))
+    W("v", k)
+    k = V(v.tensor_tensor_scan(T.s2[:], T.m2[:], T.m2[:], 0.0, OP.add, OP.max))
+    W("v", k)
+    k = V(ts(T.s2[64:128, 0:256], T.s2[64:128, 0:256], T.s2[0:64, 255:256], None, OP.add))
+    W("v", k)
+    k = V(v.transpose(T.t2[:], T.s2[:]))
+    W("v", k)
+    k = V(tt(T.rr[:], T.t2[:, 0:256:4], T.e32[:, 0:256:4], OP.mult))
+    W("v", k)
+    k = V(v.tensor_tensor_scan(T.rs[:], T.keep8[:], T.rr[:], 0.0, OP.mult, OP.add))
+    W("v", k, n64)
+    V(ts(T.d0[:, 1:16:2], T.rs[:, 7:64:8], 64.5, 5000.0, OP.is_gt, OP.mult))
+    k = V(tt(T.d1[:, 0:16:2], T.rs[:, 7:64:8], T.n64[:], OP.add))
+    W("v", k)
+    k = V(v.tensor_tensor_scan(T.sw[:], T.d0[:], T.d1[:], 0.0, OP.add, OP.min))
+    W("v", k)
+    k = V(v.tensor_copy(T.sc[:], T.sw[:, 1:16:2]))
+    W("v", k, D["sv"], wi)
+    sca = V(v.tensor_copy(T.win[:, 16:656].indirect(T.sc[:, 0:8]), T.vals[:]))
+
+    def offsets(h):
+        o, a, b = 544 * h, 32 * h, 32 * h + 17
+        V(v.transpose(T.tt[:, o:o + 256], T.win[:, 16 + 256 * h:272 + 256 * h]))
+        k = V(v.transpose(T.tt[:, o + 256:o + 544], T.win[:, 256 * h:256 * h + 288]))
+        W("v", k)
+        V(tt(T.wa[:, a:b], T.tt[:, o:o + 544:32], T.tt[:, o + 16:o + 544:32], OP.min))
+        for r in (0, 64):
+            k = V(tt(T.wb[64 - r:128 - r, a:b], T.tt[r:r + 64, o:o + 544:32], T.tt[r:r + 64, o + 16:o + 544:32], OP.min))
+        W("v", k)
+        k = V(tt(T.wm[:, a:b], T.wa[:, a:b], T.wb[:, a:b], OP.min))
+        W("v", k)
+        k = V(ts(T.offs2[:, 16 * h:16 * h + 16], T.wm[:, a:b].indirect(T.offx[:, 4:5]), 256.0, None, OP.add))
+        W("v", k)
+        W("s", k)
+    W("v", sca)
+    offsets(0)
     c2r = pickc("sl2r", 0, 256, "hq", 514, "offs2", 0, 16)
     s2r = picks("sl2r", 0, 256, "hq", 514, "offs2", 0, 16)
+    offsets(1)
     c2d = pickc("sl2d", 0, 192, "hq", 514, "offs2", 16, 28)
     s2d = picks("sl2d", 0, 192, "hq", 514, "offs2", 16, 28)
-    k = V(v.tensor_tensor(T.ia[:], T.tt[:, 1:512:16], T.tt[:, 2:512:16], OP.add))
+    for r in range(2):
+        k = V(v.tensor_tensor_scan(T.ia[0:64, 128 * r:128 * r + 100], T.keep4[64 * r:64 * r + 64, 0:100], T.tt[64 * r:64 * r + 64, 1:800:8],
+                                   0.0, OP.mult, OP.add))
+    W("v", k)
+    k = V(tt(T.ib[0:64, 0:25], T.ia[0:64, 3:100:4], T.ia[0:64, 131:228:4], OP.add))
+    W("v", k)
+    idr = V(v.tensor_copy(T.idm[0:64, 0:8], T.ib[0:64, 0:8]))
+    idd = V(v.tensor_copy(T.idm[0:64, 8:16], T.ib[0:64, 17:25]))
+    ido = V(v.tensor_copy(T.idl[0:64, 8 * me:8 * me + 2], T.ib[0:64, 23:25]))
     c2o = pickc("hl", own, own + 64, "hq", 514, "offs2", 28, 32)
     s2o = picks("hl", own, own + 64, "hq", 514, "offs2", 28, 32)
-    W("v", k)
-    k = V(v.tensor_tensor(T.ib[:], T.ia[:, 0:32:2], T.ia[:, 1:32:2], OP.add))
-    W("v", k)
-    idm = V(v.tensor_copy(T.idm[:], T.ib[:]))
-    ido = V(v.tensor_copy(T.idl[:, 8 * me:8 * me + 2], T.ib[:, 14:16]))
+    qw = quant("wq", "wt", 0, 128, ldw)
     W("g", c2r)
-    fused(far_parts(lambda i: u8("sl2rc", 64 * i, 64 * i + 64), u8("r2c", 0, 64), "rc2"))
+    fused([(rl[1 + i], all_[8 * i:8 * i + 8], u8("sl2rc", 128 * i, 128 * i + 128), u8("r2c", 0, 128), "rc2") for i in range(2)])
     W("g", s2r)
-    fused(far_parts(lambda i: T.sl2rs[:, 64 * i:64 * i + 64], T.r2s[:, 0:64], "rs2"))
+    fused([(rl[3 * i], all_[8 * i:8 * i + 8], T.sl2rs[:, 128 * i:128 * i + 128], T.r2s[:, 0:128], "rs2") for i in range(2)])
     W("g", c2d)
-    fused(near_parts(lambda i: u8("sl2dc", 64 * i, 64 * i + 64), u8("hlc", own, own + 64), "a2"))
+    fused([(C[dof[4 + i]], shares(out_, i), u8("sl2dc", 64 * i, 64 * i + 64), u8("hlc", own, own + 64), "a2") for i in range(3)])
     W("g", s2d)
-    fused(near_parts(lambda i: T.sl2ds[:, 64 * i:64 * i + 64], T.hls[:, own:own + 64], "a2", True))
-    W("g", idm)
-    fused(far_parts(lambda i: T.idm[:, 2 * i:2 * i + 2], T.r2l[:, 0:2], "rl2", True))
-    fused(near_parts(lambda i: T.idm[:, 8 + 2 * i:10 + 2 * i], T.idl[:, 8 * me:8 * me + 2], "l2"))
+    fused([(C[dof[4 + i]], shares(out_, i, True), T.sl2ds[:, 64 * i:64 * i + 64], T.hls[:, own:own + 64], "a2") for i in range(3)])
+    W("g", idr)
+    fused([(rl[3 * i], in_[4 * i:4 * i + 4], T.idm[:, 4 * i:4 * i + 4], T.r2l[:, 0:4], "rl2") for i in range(2)])
+    W("g", idd)
+    for i in range(3):
+        fused([(C[dof[4 + i]], out_, T.idm[:, 8 + 2 * i:10 + 2 * i], T.idl[:, 8 * me:8 * me + 2], "l2")])
 
-    arr = [("a2", nd + 2 * nf), c2o, s2o]
-    D["mY0"] = product("Y0", 256, "wq", 0, "hl", 0, *arr)
+    arr = [("a2", nd + nf), c2o, s2o]
+    D["mY0"] = product("Y0", 256, "wq", 0, "hl", 0, qw, *arr)
     D["mY1"] = product("Y1", 256, "wq", 0, "hl", 256)
     W("y", *arr)
     load("y", "st", T.oc[:, 0:2048], u8("hlc", 0, 512))
-    W("s", *arr)
     for b in range(4):
-        load("s", "sts", T.osc[4 * b:4 * b + 4, 0:512], T.hls[32 * b:32 * b + 4, 0:512])
+        load("y", "st", T.osc[4 * b:4 * b + 4, 0:512], T.hls[32 * b:32 * b + 4, 0:512])
     k0 = leave("Y0", "s", T.ysb[:, 0:256], 256, AF.Copy, 1.0)
     k1 = leave("Y1", "v", T.ysb[:, 256:512], 256, AF.Copy, 1.0)
-    W("y", k0, k1)
-    st = load("y", "st", T.y[:], T.ysb[:])
-    W("v", ("l2", ndl + nf), ido)
+    W("s", k0, k1)
+    load("s", "sts", T.y[:], T.ysb[:])
+    st = ("st", cnt["st"])
+    W("v", ("l2", 3 * len(out_) + nf // 2), ido)
     for h in range(2):
-        k = V(v.tensor_scalar(T.idf[:, h:16:2], T.idl[:, h:64:8], -1.0, None, OP.add))
+        k = V(ts(T.idf[0:32, h:16:2], T.idl[0:32, h:64:8], -1.0, None, OP.add))
     W("v", k)
-    k = V(v.transpose(T.idt[:], T.idf[:]))
+    k = V(v.transpose(T.idt[0:32, 0:32], T.idf[0:32, 0:32]))
     W("s", k)
     sts = load("s", "sts", T["id"][0:1, 0:512], T.idt[0:16, 0:32])
     W("y", st)

from concourse.bass import DstId, RemoteDMATransfer
from concourse.mybir import dt, AluOpType as OP, ActivationFunctionType as AF

F8, U8, BF, F32, U16, I32 = "float8_e4m3fn_x4", "uint8", "bfloat16", "float32", "uint16", "int32"
SCRATCH = {"ps": ("psum", [128, 4096], F32)}
for _n, _w in (("xq", 130), ("plq", 128), ("plp", 128), ("p2q", 128), ("p2p", 128), ("wq", 128), ("wvq", 512), ("sl1r", 256),
               ("sl1d", 128), ("cl", 512), ("cp", 512), ("vq", 512), ("aq", 512), ("hq", 640), ("sl2r", 256), ("sl2d", 192),
               ("hl", 512), ("xl", 256), ("r0", 32), ("r1", 64), ("r2", 128)):
    SCRATCH[_n + "c"] = ("sbuf", [128, _w], F8)
    SCRATCH[_n + "s"] = ("sbuf", [128, _w], U8)
for _t, _b in ((BF, "xt 520 plt 512 p2t 512 wt 512 wvt 2048 zt 656 vt 2048 at 2048 ht 2048 vals 128 nb1 16 ns1 16 e1 128 m1 128 "
                    "s1 128 jS 1024 jV 1024 jW 1024 lst1 16 ll1 64 lwb 4 lwt 16 nb2 32 ns2 32 e32 256 m2 256 s2 256 t2 256 rr 64 "
                    "rs 64 hd 64 keep4 128 keep8 64 win 656 tt 1088 wa 64 wb 64 wm 64 vin 256 vtr 256 r1l 2"),
               (F32, "cf 12 ci0 48 thr 8 kc1 128 kc8 64 ic 32 iv 32 cg 16 tz1 128 tz2 256 "
                     "xr 16 x1 32 x1t 32 d0 16 d1 16 sw 16 n64 8 ia 256 ib 32 idf 32 idt 32 ysb 512"),
               (U16, "rep1 8 rep8 4 offp 8 offc 32 offs1 32 sc 8 offs2 32 offv 8 offx 12 offw 4 idm 16 idl 64 r0l 4 r2l 4"),
               (I32, "pI 2 ci 12")):
    _b = _b.split()
    for _i in range(0, len(_b), 2):
        SCRATCH[_b[_i]] = ("sbuf", [128, int(_b[_i + 1])], _t)
SEMAPHORES = ("pv psc pt pg ldx ldpl ldwv ldp2 ldw a0 l0 a1 l1 a2 l2 ls st sts rc0 rs0 rl0 rc1 rs1 rl1 rc2 rs2 rl2").split()

ORDER = ("pc0 pp0 mV00 mA00 mA01 pc1 pp1 mV30 eV00:s mV20 eV20:s eA00:v eA01:v mV10 mA10 eV30:v mA30 eV10:v eA30:v mA20 mA11 "
         "eA10:s qV1 mA21 eA20:s mA31 qA0 eA11:s sm mO30 eA31:s qV0 eO30:s eA21:v mO20 tv mO10 mO00 qA1 mO21 eO20:s eO10:v mO01 "
         "qA2 eO01:v mO11 mO12 eO21:v eO00:s mO31 mO02 eO12:v mO22 eO11:v eO31:s qH0 eO02:s mO32 eO22:v eO32:s mZ0 qH1 mZ1 qH2 "
         "eZ0 mZ2 sv eZ1 eZ2").split()
PIECES = ((0, 256), (256, 384), (384, 512))


def kmap(topo, cores, s):
    far = [d for d in range(8) if d != s and not topo.may_write(cores[s], cores[d])]
    for w in ((1, 2, 4), (1, 4, 2), (2, 1, 4), (2, 4, 1), (4, 1, 2), (4, 2, 1)):
        for f in range(8):
            k = [sum(w[b] * ((d >> b ^ f >> b) & 1) for b in range(3)) for d in range(8)]
            if k[s] == 7 and all(k[d] < 4 for d in far):
                return w, f, k, [k.index(i) for i in range(8)], far
    raise ValueError("no order of the destinations")


def relays(topo, cores, s):
    far = kmap(topo, cores, s)[4]
    r = [c for c in topo.cores_of(cores[s]) if c != cores[s] and all(topo.may_write(c, cores[d]) for d in far)]
    here = [c for c in r if topo.die(c) == topo.die(cores[s])]
    return here[:1] + [c for c in r if c not in here] + here[1:]


def bits(es):
    return sum(1 << e for e in es)


def shares(es, i, turned=False):
    return ((es[0:4], es[4:6], es[6:8]) if turned else (es[0:2], es[2:4], es[4:8]))[i]


def relay_program(g, core, T, topo):
    C = T.cores
    for s in range(8):
        if core not in topo.cores_of(C[s]):
            continue
        rl = relays(topo, C, s)
        if core not in rl[:4]:
            continue
        i = rl.index(core)
        dof = kmap(topo, C, s)[3]
        n = [0]

        def go(sem, m, out, src, rsem, d):
            rid, pid = topo.addr(C[d], core)
            es = topo.engines(core, C[d])
            g.wait_ge(T.sem[sem], m)
            g.remote_dma(out, src, T.sem[rsem], T.sem.ls, pid, rid, bits(es))
            n[0] += len(es)

        def two(sem, m, out, src, rsem):
            g.wait_ge(T.sem[sem], m)
            tr = []
            for h in range(2):
                d = dof[2 * (i // 2) + h]
                rid, pid = topo.addr(C[d], core)
                es = topo.engines(core, C[d])[4 * h:4 * h + 4]
                tr.append(RemoteDMATransfer(dst_ids=[DstId(rid=rid, pnc=pid)], dma_engine_mask=bits(es), remote_sem=T.sem[rsem], srcs=[src(h)], dsts=[out]))
                n[0] += len(es)
            g.remote_dma_fused(tr, local_sem=T.sem.ls)
        a, b = 64 * s, 64 * s + 64
        go("rc0", 4, T.xlc[:, 32 * i:32 * i + 32].bitcast(dt.uint8), T.r0c[:, 0:32].bitcast(dt.uint8), "a0", dof[0])
        go("rs0", 4, T.xls[:, 32 * i:32 * i + 32], T.r0s[:, 0:32], "a0", dof[0])
        if i == 0:
            go("rl0", 8, T.offw[:, 0:4], T.r0l[:, 0:4], "l0", dof[0])
        else:
            go("rc1", 4, T.clc[:, a:b].bitcast(dt.uint8), T.r1c[:, 0:64].bitcast(dt.uint8), "a1", dof[i])
            go("rs1", 4, T.cls[:, a:b], T.r1s[:, 0:64], "a1", dof[i])
            go("rl1", len(shares(list(range(8)), i - 1)), T.ll1[:, 8 * s:8 * s + 2], T.r1l[:, 0:2], "l1", dof[i])
        if i in (1, 2):
            two("rc2", 8, T.hlc[:, a:b].bitcast(dt.uint8), lambda h: T.r2c[:, 64 * h:64 * h + 64].bitcast(dt.uint8), "a2")
        else:
            two("rs2", 8, T.hls[:, a:b], lambda h: T.r2s[:, 64 * h:64 * h + 64], "a2")
            two("rl2", 4, T.idl[:, 8 * s:8 * s + 2], lambda h: T.r2l[:, 2 * h:2 * h + 2], "l2")
        g.wait_ge(T.sem.ls, n[0])


def rank_program(g, core, T, topo):
    me = T.rank_of(core)
    if me is None:
        return relay_program(g, core, T, topo)
    C = T.cores
    w3, flip, kof, dof, far = kmap(topo, C, me)
    K0 = sum(w3[b] for b in range(3) if flip >> b & 1)
    ws = [-w3[b] if flip >> b & 1 else w3[b] for b in range(3)]
    pi = sorted(range(3), key=lambda b: -w3[b])
    lam, sg = ws[pi[2]], 1 if ws[pi[0]] > 0 else -1
    d2, d3 = ws[pi[0]] // ws[pi[1]], ws[pi[1]] * lam
    F0 = 8 * d2 * d3 * (1 - sg) + 8 * d3 + 8
    rl = relays(topo, C, me)
    Q = {"v": g.vector, "s": g.scalar, "t": g.tensor, "g": g, "y": g.sync}
    SEM = {"v": "pv", "s": "psc", "t": "pt", "g": "pg"}
    cnt, seen = {}, {q: {} for q in Q}

    def W(q, *toks):
        best = {}
        for t in toks:
            best[t[0]] = max(best.get(t[0], 0), t[1])
        for sem in best:
            if seen[q].get(sem, 0) < best[sem]:
                Q[q].wait_ge(T.sem[sem], best[sem])
                seen[q][sem] = best[sem]

    def done(q, inst):
        cnt[q] = cnt.get(q, 0) + 1
        inst.then_inc(T.sem[SEM[q]], 1)
        return (SEM[q], cnt[q])

    def V(inst):
        return done("v", inst)

    def S(inst):
        return done("s", inst)

    def load(q, sem, out, in_):
        cnt[sem] = cnt.get(sem, 0) + 16
        Q[q].dma_start(out, in_).then_inc(T.sem[sem], 16)
        return (sem, cnt[sem])
    v, sc, te = g.vector, g.scalar, g.tensor
    ts, tt = v.tensor_scalar, v.tensor_tensor
    lsn = [0]

    def fused(parts):
        tr = []
        for dst, es, s_, d_, sem in parts:
            rid, pid = topo.addr(dst, core)
            tr.append(RemoteDMATransfer(dst_ids=[DstId(rid=rid, pnc=pid)], dma_engine_mask=bits(es), remote_sem=T.sem[sem], srcs=[s_], dsts=[d_]))
            lsn[0] += len(es)
        g.remote_dma_fused(tr, local_sem=T.sem.ls)

    def u8(t, a, b):
        return T[t][:, a:b].bitcast(dt.uint8)

    def pickc(out, a, b, src, n, off, e, f):
        return V(v.tensor_copy(T[out + "c"][:, a:b].bitcast(dt.uint32), T[src + "c"][:, 0:n].bitcast(dt.uint32).indirect(T[off][:, e:f])))

    def picks(out, a, b, src, n, off, e, f):
        return S(sc.activation(T[out + "s"][:, a:b], T[src + "s"][:, 0:n].indirect(T[off][:, e:f]), AF.Copy))

    def quant(n, t, a, b, *deps):
        W("v", *deps)
        return V(v.quantize_mx(T[n + "c"][:, a:b], T[n + "s"][:, a:b], T[t][:, 4 * a:4 * b]))

    def mm(out, n, l, lo, r, ro):
        return done("t", te.matmul_mx(T.ps[:, out:out + n], T[l + "c"][:, lo:lo + 128], T[l + "s"][:, lo:lo + 128],
                                      T[r + "c"][:, ro:ro + n], T[r + "s"][:, ro:ro + n], True, True))
    out_ = topo.engines(core, C[dof[4]])
    in_ = [e for e in topo.engines(core, rl[0]) if e not in out_]
    all_ = out_ + in_

    ldx = load("y", "ldx", T.xt[:, 0:512], T.x[:])
    ldpl = load("s", "ldpl", T.plt[:, 0:16], T.pl[:, 0:16])
    ldwv = load("y", "ldwv", T.wvt[:], T.wv[:])
    ldp2 = load("y", "ldp2", T.p2t[:, 0:16], T.p2[:, 0:16])

    fl = {"allow_small_or_imprecise_dtypes": True}
    three, i16 = T.ci0[:, 0:4], T.ci0[:, 32:48]
    gi = done("g", g.iota(T.pI[:, 0:1], [[0, 1]], 0, 1))
    gi1 = done("g", g.iota(three, [[0, 4]], 3, 0, **fl))
    done("g", g.iota(T.ci0[:, 8:16], [[4, 8]], 1, 0, **fl))
    done("g", g.iota(T.ci0[:, 16:24], [[4, 4], [0, 2]], 3, 0, **fl))
    gi2 = done("g", g.iota(T.kc1[:], [[0, 4], [lam, 8], [0, 4]], F0 - lam * K0, 0, **fl))
    done("g", g.iota(i16, [[1, 16]], 0, 0, **fl))
    done("g", g.iota(T.ic[:], [[1, 4], [64, 8]], 0, 0, **fl))
    done("g", g.iota(T.iv[:, 0:16], [[32, 8], [0, 2]], -256, 0, **fl))
    done("g", g.iota(T.iv[:, 16:32], [[128, 4], [0, 4]], 0, 0, **fl))
    gi3 = done("g", g.iota(T.kc8[:], [[0, 8], [lam, 8]], F0 - lam * K0, 0, **fl))
    zp = V(v.memset(T.plt[:, 16:512], 0.0))
    W("v", gi)

    def field(i, shift, mask):
        if shift:
            return V(ts(T.ci[:, i:i + 1], T.pI[:, 0:1], shift, mask, OP.arith_shift_right, OP.bitwise_and))
        return V(ts(T.ci[:, i:i + 1], T.pI[:, 0:1], mask, None, OP.bitwise_and))
    field(0, 0, 15), field(1, 0, 3), field(2, 5, 2)
    c0 = field(3, 4, 1)
    zx = V(v.memset(T.xt[:, 512:520], 0.0))
    W("v", c0)
    c0 = V(v.tensor_copy(T.cf[:, 0:4], T.ci[:, 0:4]))
    for b, x in enumerate((0, -sg, d2, d3)):
        V(v.memset(T.hd[:, b:64:4], float(x)))
    W("v", c0)
    l16, u4, h2, mO, lane, par, b3, l2, l4, l2m, h32 = (T.cf[:, i:i + 1] for i in range(11))
    cg = [T.cg[:, i:i + 1] for i in range(16)]
    V(ts(cg[0], l16, 8.0, float(pi[0] - 3), OP.is_equal, OP.mult))
    V(ts(cg[1], l16, 0.0, float(pi[1] - 3), OP.is_equal, OP.mult))
    c1 = V(ts(cg[2], l16, 8.0, float(pi[2] - 3), OP.is_equal, OP.mult))
    c2 = V(ts(cg[3], u4, 32.0, h2, OP.mult, OP.add))
    W("v", c1, gi1)
    V(ts(T.offp[:, 0:8:2], three, cg[0], None, OP.add))
    c1 = V(ts(T.offp[:, 1:8:2], three, cg[1], cg[2], OP.add, OP.add))
    W("v", c2, gi2)
    V(ts(T.thr[:], T.ci0[:, 8:16], cg[3], None, OP.add))
    V(ts(T.offx[:, 0:1], l16, 2.0, mO, OP.mult, OP.add))
    c3 = V(v.tensor_copy(T.rep1[:], T.ci0[:, 16:24]))

    qpl = quant("plq", "plt", 0, 128, ldpl, zp)
    W("v", qpl, c1)
    W("s", qpl, c1)
    ppc, pps = pickc("plp", 0, 128, "plq", 128, "offp", 0, 8), picks("plp", 0, 128, "plq", 128, "offp", 0, 8)
    qx = quant("xq", "xt", 0, 130, ldx, zx)
    W("g", qx)
    fused([(rl[i], all_[4 * i:4 * i + 4], u8("xqc", 32 * i, 32 * i + 32), u8("r0c", 0, 32), "rc0") for i in range(4)])
    fused([(rl[i], all_[4 * i:4 * i + 4], T.xqs[:, 32 * i:32 * i + 32], T.r0s[:, 0:32], "rs0") for i in range(4)])
    W("t", ppc, pps, qx)
    z = mm(0, 128, "plp", 0, "xq", 0)
    W("v", z, c3)
    z1 = V(v.transpose(T.tz1[:], T.ps[:, 0:128]))
    W("v", z1)
    k = V(ts(T.nb1[:], T.tz1[:, 0:128:8], 0.0, 8.0, OP.is_lt, OP.add))
    W("v", k)
    k = V(v.tensor_tensor_scan(T.ns1[:], T.hd[:, 0:16], T.nb1[:], 0.0, OP.mult, OP.add))
    W("v", k)
    k = V(tt(T.e1[:], T.ns1[:, 0:16].indirect(T.rep1[:, 0:8]), T.kc1[:], OP.is_equal))
    W("v", k)
    k = V(v.transpose(T.m1[:], T.e1[:]))
    W("v", k)
    k = V(v.tensor_tensor_scan(T.s1[:], T.m1[:], T.m1[:], 0.0, OP.add, OP.max))
    W("s", k)
    W("v", k)
    nS = 3
    for i in range(nS):
        ks = S(sc.activation(T.jS[:, 128 * i:128 * i + 128], T.s1[:], AF.Sign, bias=T.thr[:, i:i + 1], scale=-2.0, accum_out=T.xr[:, i:i + 1]))
    nV = 128 * (8 - nS)
    for i in range(nS, 8):
        k = V(ts(T.jV[:, 128 * (i - nS):128 * (i - nS) + 128], T.s1[:], 2.0, T.thr[:, i:i + 1], OP.mult, OP.is_gt))
    W("v", k)
    k = V(v.tensor_tensor_scan(T.jW[:, 0:nV], T.jV[:, 0:nV], T.jV[:, 0:nV], 0.0, OP.mult, OP.add))
    W("v", k)
    for a in (0, 8):
        V(ts(T.xr[:, a + nS:a + 8], T.jW[:, 127:nV:128], -2.0, 128.0, OP.mult, OP.add))
    W("v", ks)
    k = V(v.tensor_copy(T.xr[:, 8:8 + nS], T.xr[:, 0:nS]))
    W("v", k)
    for a in (0, 64):
        for b in range(2):
            k = V(v.tensor_copy(T.x1[a:a + 64, b:32:2], T.xr[64 * b:64 * b + 64, 0:16]))
    W("v", k)
    k = V(v.transpose(T.x1t[:], T.x1[:]))
    W("v", k)
    of1 = V(ts(T.offs1[:], T.x1t[:], 0.5, 64.0, OP.mult, OP.add))
    W("v", of1)
    W("s", of1)
    own = 64 * me
    c1r = pickc("sl1r", 0, 256, "xq", 130, "offs1", 4, 20)
    s1r = picks("sl1r", 0, 256, "xq", 130, "offs1", 4, 20)
    c1d = pickc("sl1d", 0, 128, "xq", 130, "offs1", 20, 28)
    s1d = picks("sl1d", 0, 128, "xq", 130, "offs1", 20, 28)
    l1 = V(ts(T.lst1[:], T.x1t[:, 0:32].indirect(T.offx[:, 0:1]), 0.5, 64.0, OP.mult, OP.add))
    c1o = pickc("cl", own, own + 64, "xq", 130, "offs1", 28, 32)
    s1o = picks("cl", own, own + 64, "xq", 130, "offs1", 28, 32)

    W("g", of1)
    fused([(rl[0], in_, T.offs1[:, 0:4], T.r0l[:, 0:4], "rl0")])
    W("g", c1r)
    fused([(rl[i], all_[4 * i:4 * i + 4], u8("sl1rc", 64 * i - 64, 64 * i), u8("r1c", 0, 64), "rc1") for i in range(1, 4)]
          + [(C[dof[4]], out_[0:4], u8("sl1rc", 192, 256), u8("clc", own, own + 64), "a1")])
    W("g", s1r)
    fused([(rl[i], all_[4 * i:4 * i + 4], T.sl1rs[:, 64 * i - 64:64 * i], T.r1s[:, 0:64], "rs1") for i in range(1, 4)]
          + [(C[dof[4]], out_[0:4], T.sl1rs[:, 192:256], T.cls[:, own:own + 64], "a1")])
    W("g", c1d)
    fused([(C[dof[5 + i]], out_[4 * i:4 * i + 4], u8("sl1dc", 64 * i, 64 * i + 64), u8("clc", own, own + 64), "a1") for i in range(2)])
    W("g", s1d)
    fused([(C[dof[5 + i]], out_[4 * i:4 * i + 4], T.sl1ds[:, 64 * i:64 * i + 64], T.cls[:, own:own + 64], "a1") for i in range(2)])
    W("g", l1)
    fused([(rl[i], shares(in_, i - 1), T.lst1[:, 2 * i:2 * i + 2], T.r1l[:, 0:2], "rl1") for i in range(1, 4)])
    fused([(C[dof[4 + i]], shares(out_, i), T.lst1[:, 8 + 2 * i:10 + 2 * i], T.ll1[:, 8 * me:8 * me + 2], "l1") for i in range(3)])

    W("v", gi3, l1)
    V(v.memset(T.zt[:], 0.0))
    field(4, 0, 31), field(5, 0, 1), field(6, 3, 1), field(7, 1, 7), field(8, 2, 3), field(9, 1, 3), field(10, 1, 32)
    V(v.tensor_copy(T.ll1[:, 8 * me:8 * me + 2], T.lst1[:, 14:16]))
    V(ts(T.offx[:, 2:3], T.offx[:, 0:1], 3.0, None, OP.min))
    V(ts(T.keep4[:], T.kc1[:], -1000.0, None, OP.is_ge))
    V(ts(cg[4], l16, 4.0, None, OP.mult))
    V(ts(cg[5], l16, 0.0, 256.0, OP.is_equal, OP.mult))
    V(ts(cg[6], mO, -17.0, 9.0, OP.mult, OP.add))
    k = V(ts(cg[7], mO, 8.0, None, OP.mult))
    W("v", k)
    W("s", k)
    zv = S(sc.activation(T.vin[:], T.zt[:, 0:256], AF.Copy))
    zp2 = S(sc.activation(T.p2t[:, 16:512], T.zt[:, 0:496], AF.Copy))
    S(sc.activation(T.e32[:], T.zt[:, 0:256], AF.Copy))
    wi = S(sc.activation(T.win[:], T.zt[:], AF.Identity, bias=cg[5]))
    k = V(v.tensor_copy(T.cf[:, 4:11], T.ci[:, 4:11]))
    V(v.quantize_mx(T.xlc[:, 128:256], T.xls[:, 128:256], T.zt[:, 0:512]))
    V(v.quantize_mx(T.hqc[:, 512:640], T.hqs[:, 512:640], T.zt[:, 0:512]))
    W("v", k)
    V(ts(T.offc[:], T.ic[:], cg[4], None, OP.add))
    V(ts(cg[8], b3, 4.0, 3.0, OP.mult, OP.add))
    V(ts(cg[9], par, cg[6], cg[7], OP.mult, OP.add))
    V(ts(cg[10], l4, 6.0, l2, OP.mult, OP.add))
    V(ts(cg[11], l2m, 8.0, par, OP.mult, OP.add))
    V(ts(cg[12], h32, 8.0, lane, OP.mult, OP.add))
    V(ts(cg[13], h32, 16.0, None, OP.mult))
    V(ts(cg[14], l16, 512.0, None, OP.add))
    V(ts(T.offv[:], T.ci0[:, 32:40], 32.0, lane, OP.mult, OP.add))
    V(ts(T.keep8[:], T.kc8[:], float(F0 - lam * K0), None, OP.not_equal))
    V(v.memset(T.keep4[:, 0:128:4], 0.0))
    V(v.memset(T.d0[:, 0:16:2], 1000000.0))
    V(v.memset(T.idf[0:32, 16:32], 0.0))
    k = V(v.memset(T.idm[64:128, 0:16], 0))
    W("v", k, zv)
    V(ts(T.rep8[:], T.ci0[:, 32:36], 8.0, cg[8], OP.mult, OP.add))
    V(ts(T.offx[:, 4:5], cg[9], l2, None, OP.add))
    V(ts(T.offx[:, 6:7], cg[10], h32, None, OP.add))
    V(ts(T.offx[:, 8:9], cg[11], h32, None, OP.add))
    V(ts(T.vin[:, 0:256:16], T.iv[:, 0:16], cg[12], None, OP.add))
    V(ts(T.vin[:, 9:256:16], T.iv[:, 16:32], cg[13], None, OP.add))
    V(ts(T.d1[:, 1:16:2], T.ci0[:, 32:40], 16.0, cg[14], OP.mult, OP.add))
    k = quant("p2q", "p2t", 0, 128, ldp2, zp2)
    qwv = quant("wvq", "wvt", 0, 512, ldwv)
    W("v", k)
    W("s", k)
    p2c, p2s = pickc("p2p", 0, 128, "p2q", 128, "offp", 0, 8), picks("p2p", 0, 128, "p2q", 128, "offp", 0, 8)

    ks_ = [kmap(topo, C, s)[2][me] for s in range(8)]
    s0 = ks_.index(0)
    ne = [len(topo.engines(relays(topo, C, s)[ks_[s]], core)) if s in far else 0 for s in range(8)]
    W("v", ("a0", 8 * ne[s0]), ("l0", ne[s0]), p2c)
    W("s", ("a0", 8 * ne[s0]), ("l0", ne[s0]), p2c)
    c0o = pickc("cl", 64 * s0, 64 * s0 + 64, "xl", 130, "offw", 0, 4)
    s0o = picks("cl", 64 * s0, 64 * s0 + 64, "xl", 130, "offw", 0, 4)
    k = V(v.tensor_copy(T.lwb[:], T.offw[:]))
    W("v", k)
    k = V(v.tensor_copy(T.lwt[:], T.lwb[:, 0:4].indirect(T.offx[:, 2:3])))
    W("v", k)
    l0 = V(v.tensor_copy(T.ll1[:, 8 * s0:8 * s0 + 2], T.lwt[:, 0:2]))

    nf = sum(ne)
    nl = sum(len(shares(out_, ks_[s] - 4)) for s in range(8) if 4 <= ks_[s] < 7)
    nd = nl + sum(len(shares(out_, ks_[s] - 4, True)) for s in range(8) if 4 <= ks_[s] < 7)
    a1 = ("a1", 24 + 2 * (nf - ne[s0]))
    W("v", a1, c1o, s1o, c0o, s0o)
    W("s", a1, c1o, s1o, c0o, s0o)
    W("t", a1, c1o, s1o, c0o, s0o)
    W("y", a1)
    ldw = load("y", "ldw", T.wt[:], T.w[:])
    D, bank, users = {}, {}, [z1] + [None] * 7

    def product(x, n, l, lo, r, ro, *deps):
        b = len(bank) % 8
        W("t", *(list(deps) + ([users[b]] if users[b] else [])))
        bank[x] = b
        return mm(512 * b, n, l, lo, r, ro)

    def leave(x, q, out, n, func, scale):
        src = T.ps[:, 512 * bank[x]:512 * bank[x] + n]
        W(q, D["m" + x])
        if q == "s":
            k = S(sc.activation(out, src, func, scale=scale))
        elif func == AF.Relu:
            k = V(ts(out, src, 0.0, scale, OP.max, OP.mult))
        else:
            k = V(v.tensor_copy(out, src) if scale == 1.0 else ts(out, src, scale, None, OP.mult))
        users[bank[x]] = k
        return k

    for x in ORDER:
        x, q = (x + ":").split(":")[:2]
        j = int(x[-1]) if x[-1] in "0123" else 0
        a, b = PIECES[j]
        p0, p1 = 256 * j, 256 * j + 256
        if x[:2] in ("pc", "pp"):
            D[x] = (pickc if x[1] == "c" else picks)("cp", 128 * j, 128 + 384 * j, "cl", 512, "offc", 8 * j, 8 + 24 * j)
        elif x[:2] in ("mV", "mA"):
            t = int(x[2])
            D[x] = product(x[1:], 512 if x[1] == "V" else 256, "cp", 128 * t, "wvq" if x[1] == "V" else "cl", p0,
                           D["pc%d" % min(t, 1)], D["pp%d" % min(t, 1)])
        elif x[:2] == "eV":
            D[x] = leave(x[1:], q, T.vt[:, int(x[2]):2048:4], 512, AF.Copy, 1.0)
        elif x[:2] == "eA":
            D[x] = leave(x[1:], q, T["at"][:, 4 * p0 + int(x[2]):4 * p1:4], 256, AF.Relu, 0.0625)
        elif x[:2] == "qV":
            D[x] = quant("vq", "vt", p0, p1, *[D["eV%d0" % t] for t in range(4)])
        elif x[:2] == "qA":
            D[x] = quant("aq", "at", a, b, *[D["eA%d%d" % (t, a // 256)] for t in range(4)])
        elif x[:2] == "mO":
            D[x] = product(x[1:], b - a, "vq", 128 * int(x[2]), "aq", a, D["qA%d" % j], D["qV%d" % (int(x[2]) // 2)])
        elif x[:2] == "eO":
            D[x] = leave(x[1:], q, T.ht[:, 4 * a + int(x[2]):4 * b:4], b - a, AF.Copy, 0.0625)
        elif x[:2] == "qH":
            D[x] = quant("hq", "ht", a, b, *[D["eO%d%d" % (i, j)] for i in range(4)])
        elif x[:2] == "mZ":
            D[x] = product(x[1:], b - a, "p2p", 0, "hq", a, D["qH%d" % j])
        elif x[:2] == "eZ":
            W("v", D["m" + x[1:]])
            r, o = 64 * (a // 256), 512 * bank[x[1:]]
            D[x] = users[bank[x[1:]]] = V(v.transpose(T.tz2[r:r + 64, a % 256:a % 256 + b - a], T.ps[r:r + 64, o:o + b - a]))
        elif x == "sm":
            W("s", ("l1", nl + nf - ne[s0]), l0)
            S(sc.activation(T.vin[:, 1:256:16], T.ll1[:, 0:64].indirect(T.offx[:, 6:7]), AF.Identity, bias=1.0))
            D[x] = S(sc.activation(T.hd[:, 1:64:4], T.ll1[:, 0:64].indirect(T.offx[:, 8:9]), AF.Sign, bias=-127.5 * sg, scale=float(sg)))
        elif x == "tv":
            W("v", D["sm"])
            D[x] = V(v.transpose(T.vtr[:], T.vin[:]))
        else:
            W("s", D["tv"])
            D[x] = S(sc.activation(T.vals[:], T.vtr[:, 0:256].indirect(T.offv[:, 0:8]), AF.Copy))
    W("v", D["eZ2"])
    k = V(ts(T.nb2[:], T.tz2[:, 0:256:8], 0.0, 8.0, OP.is_lt, OP.add))
    W("v", k)
    k = V(v.tensor_tensor_scan(T.ns2[:], T.hd[:, 0:32], T.nb2[:], 0.0, OP.mult, OP.add))
    W("v", k)
    W("s", k)
    n64 = S(sc.activation(T.n64[:], T.ns2[:, 3:32:4], AF.Identity, bias=64.0 * (K0 - lam * F0) - 1.0, scale=64.0 * lam))
    k = V(tt(T.e32[:, 0:256:4], T.ns2[:, 0:32].indirect(T.rep8[:, 0:4]), T.kc8[:], OP.is_equal))
    W("v", k)
    k = V(v.transpose(T.m2[:], T.e32[:]))
    W("v", k)
    k = V(v.tensor_tensor_scan(T.s2[:], T.m2[:], T.m2[:], 0.0, OP.add, OP.max))
    W("v", k)
    k = V(ts(T.s2[64:128, 0:256], T.s2[64:128, 0:256], T.s2[0:64, 255:256], None, OP.add))
    W("v", k)
    k = V(v.transpose(T.t2[:], T.s2[:]))
    W("v", k)
    k = V(tt(T.rr[:], T.t2[:, 0:256:4], T.e32[:, 0:256:4], OP.mult))
    W("v", k)
    k = V(v.tensor_tensor_scan(T.rs[:], T.keep8[:], T.rr[:], 0.0, OP.mult, OP.add))
    W("v", k, n64)
    V(ts(T.d0[:, 1:16:2], T.rs[:, 7:64:8], 64.5, 5000.0, OP.is_gt, OP.mult))
    k = V(tt(T.d1[:, 0:16:2], T.rs[:, 7:64:8], T.n64[:], OP.add))
    W("v", k)
    k = V(v.tensor_tensor_scan(T.sw[:], T.d0[:], T.d1[:], 0.0, OP.add, OP.min))
    W("v", k)
    k = V(v.tensor_copy(T.sc[:], T.sw[:, 1:16:2]))
    W("v", k, D["sv"], wi)
    sca = V(v.tensor_copy(T.win[:, 16:656].indirect(T.sc[:, 0:8]), T.vals[:]))

    def offsets(h):
        o, a, b = 544 * h, 32 * h, 32 * h + 17
        V(v.transpose(T.tt[:, o:o + 256], T.win[:, 16 + 256 * h:272 + 256 * h]))
        k = V(v.transpose(T.tt[:, o + 256:o + 544], T.win[:, 256 * h:256 * h + 288]))
        W("v", k)
        V(tt(T.wa[:, a:b], T.tt[:, o:o + 544:32], T.tt[:, o + 16:o + 544:32], OP.min))
        for r in (0, 64):
            k = V(tt(T.wb[64 - r:128 - r, a:b], T.tt[r:r + 64, o:o + 544:32], T.tt[r:r + 64, o + 16:o + 544:32], OP.min))
        W("v", k)
        k = V(tt(T.wm[:, a:b], T.wa[:, a:b], T.wb[:, a:b], OP.min))
        W("v", k)
        k = V(ts(T.offs2[:, 16 * h:16 * h + 16], T.wm[:, a:b].indirect(T.offx[:, 4:5]), 256.0, None, OP.add))
        W("v", k)
        W("s", k)
    W("v", sca)
    offsets(0)
    c2r = pickc("sl2r", 0, 256, "hq", 514, "offs2", 0, 16)
    s2r = picks("sl2r", 0, 256, "hq", 514, "offs2", 0, 16)
    offsets(1)
    c2d = pickc("sl2d", 0, 192, "hq", 514, "offs2", 16, 28)
    s2d = picks("sl2d", 0, 192, "hq", 514, "offs2", 16, 28)
    for r in range(2):
        k = V(v.tensor_tensor_scan(T.ia[0:64, 128 * r:128 * r + 100], T.keep4[64 * r:64 * r + 64, 0:100], T.tt[64 * r:64 * r + 64, 1:800:8],
                                   0.0, OP.mult, OP.add))
    W("v", k)
    k = V(tt(T.ib[0:64, 0:25], T.ia[0:64, 3:100:4], T.ia[0:64, 131:228:4], OP.add))
    W("v", k)
    idr = V(v.tensor_copy(T.idm[0:64, 0:8], T.ib[0:64, 0:8]))
    idd = V(v.tensor_copy(T.idm[0:64, 8:16], T.ib[0:64, 17:25]))
    ido = V(v.tensor_copy(T.idl[0:64, 8 * me:8 * me + 2], T.ib[0:64, 23:25]))
    c2o = pickc("hl", own, own + 64, "hq", 514, "offs2", 28, 32)
    s2o = picks("hl", own, own + 64, "hq", 514, "offs2", 28, 32)
    qw = quant("wq", "wt", 0, 128, ldw)
    W("g", c2r)
    fused([(rl[1 + i], all_[8 * i:8 * i + 8], u8("sl2rc", 128 * i, 128 * i + 128), u8("r2c", 0, 128), "rc2") for i in range(2)])
    W("g", s2r)
    fused([(rl[3 * i], all_[8 * i:8 * i + 8], T.sl2rs[:, 128 * i:128 * i + 128], T.r2s[:, 0:128], "rs2") for i in range(2)])
    W("g", c2d)
    fused([(C[dof[4 + i]], shares(out_, i), u8("sl2dc", 64 * i, 64 * i + 64), u8("hlc", own, own + 64), "a2") for i in range(3)])
    W("g", s2d)
    fused([(C[dof[4 + i]], shares(out_, i, True), T.sl2ds[:, 64 * i:64 * i + 64], T.hls[:, own:own + 64], "a2") for i in range(3)])
    W("g", idr)
    fused([(rl[3 * i], in_[4 * i:4 * i + 4], T.idm[:, 4 * i:4 * i + 4], T.r2l[:, 0:4], "rl2") for i in range(2)])
    W("g", idd)
    for i in range(3):
        fused([(C[dof[4 + i]], out_, T.idm[:, 8 + 2 * i:10 + 2 * i], T.idl[:, 8 * me:8 * me + 2], "l2")])

    arr = [("a2", nd + nf), c2o, s2o]
    D["mY0"] = product("Y0", 256, "wq", 0, "hl", 0, qw, *arr)
    D["mY1"] = product("Y1", 256, "wq", 0, "hl", 256)
    W("y", *arr)
    load("y", "st", T.oc[:, 0:2048], u8("hlc", 0, 512))
    for b in range(4):
        load("y", "st", T.osc[4 * b:4 * b + 4, 0:512], T.hls[32 * b:32 * b + 4, 0:512])
    k0 = leave("Y0", "s", T.ysb[:, 0:256], 256, AF.Copy, 1.0)
    k1 = leave("Y1", "v", T.ysb[:, 256:512], 256, AF.Copy, 1.0)
    W("s", k0, k1)
    load("s", "sts", T.y[:], T.ysb[:])
    st = ("st", cnt["st"])
    W("v", ("l2", 3 * len(out_) + nf // 2), ido)
    for h in range(2):
        k = V(ts(T.idf[0:32, h:16:2], T.idl[0:32, h:64:8], -1.0, None, OP.add))
    W("v", k)
    k = V(v.transpose(T.idt[0:32, 0:32], T.idf[0:32, 0:32]))
    W("s", k)
    sts = load("s", "sts", T["id"][0:1, 0:512], T.idt[0:16, 0:32])
    W("y", st)
    W("s", sts)
    W("g", ("ls", lsn[0]), ("pv", cnt["v"]), ("psc", cnt["s"]), ("pt", cnt["t"]), ("pg", cnt["g"]))
